import numpy as np, ml_dtypes
CORES = [24,25,26,27,28,29,30,31]
N = 8
BF = ml_dtypes.bfloat16
def gentries(a):
    return np.ascontiguousarray(a.reshape(8, 16, -1).transpose(0, 2, 1)).reshape(8, -1)
def gtable(e):
    e = np.asarray(e); return np.ascontiguousarray(e.reshape(8, -1, 16).transpose(0, 2, 1)).reshape(128, -1).astype(np.int32)
I, L, S, T, H, R = 3328, 256, 2, 5, 11, 2
M = L // S
W = I + R * (L + M)
def pack(F, sel, P):
    return {"front": np.ascontiguousarray(F.reshape(N, 128, I)).astype(np.float32).astype(BF), "sel0": np.ascontiguousarray(sel).astype(np.int32), "par": np.stack([gtable(a.reshape(8, -1)) for a in P])}
def rows8(rng):
    return (np.argsort(rng.random((8, 16)), axis=1) < 8)[None, :, :, None]
def of_class(rng, cl, want, n):
    order = np.argsort(cl + 0.5 * rng.random(cl.shape), axis=-1)
    cnt = np.stack([np.add.reduce((cl == c).astype(np.int64), axis=-1) for c in range(n)], axis=-1)
    first = np.add.accumulate(cnt, axis=-1) - cnt; w = want.reshape(N, 8, -1)
    at = np.take_along_axis(first, w, 2) + (np.take_along_axis(cnt, w, 2) * rng.random(w.shape)).astype(np.int64)
    return np.take_along_axis(order, np.minimum(at, I - 1), 2).reshape(want.shape)
def setup_inputs(rng):
    hi = rows8(rng); share = rng.choice(np.array([0.06, 0.12, 0.2]), (N, 8, 1))
    cl = np.where(rng.random((N, 8, I)) < share, 0, 1 + rng.integers(0, 2, (N, 8, I)))
    u = rng.random((N, 8, 16, I)); c = cl[:, :, None, :]
    F = np.where((c > 0) & ((c == 1) == hi), 128 + 128 * u, np.where(c == 0, 64 * u, 101 * u)).astype(np.int64)
    y = rng.random((N, 8, I)); sel = of_class(rng, cl, np.where((cl == 0) | (y < 0.15), 0, np.where(y < 0.2, 3 - cl, cl)), 3)
    free = rng.permutation(8) < 2; F = np.where(free[None, :, None, None], (256 * u).astype(np.int64), F)
    return pack(F, sel, rng.integers(0, I, (N, 8, L, 16)))
def setup_inputs_spread(rng):
    a = np.exp2(8 * rng.random((N, 8, 16, I))); b = np.exp2(8 * rng.random((N, 8, 1, I))) * rng.random((N, 8, 16, I))
    even = (rng.permutation(8) < 5)[None, :, None, None]
    F = np.minimum(np.where(even, a, b).astype(np.int64), 255) * (rng.random((N, 8, 1, I)) > 0.0625)
    low = (rng.permutation(8) < 4)[None, :, None]
    v = (I * rng.random((N, 8, I)) ** 3).astype(np.int64); sel = np.where(low, v, I - 1 - v)
    w = (I * rng.random((N, 8, L, 16)) ** 2).astype(np.int64); P = np.where(low[..., None], I - 1 - w, w)
    return pack(F, sel, P)
def setup_inputs_ends(rng):
    hi = rows8(rng); up = np.where(hi, np.add.accumulate(hi.astype(np.int64), axis=2), np.add.accumulate((~hi).astype(np.int64), axis=2)) - 1
    cl = rng.choice(np.array([0, 1, 1, 1, 2, 2, 2]), (N, 8, I))
    cl[..., [0, 1]] = 2; cl[..., I - 1] = 1; cl[..., [2, 3, I - 2]] = 3; cl[..., [4, 5, I - 3]] = 0
    off = rng.integers(0, 8, (2, N, 8, 1, I)); off[..., [0, 1, I - 1]] = 8; c = cl[:, :, None, :]
    F = 255 * ((c == 3) | ((c > 0) & ((c == 1) == hi) & (up != off[0]) & (up != off[1]))).astype(np.int64)
    F[..., 1] = np.where((~hi & (up == 7))[..., 0], 254, F[..., 1]); F[:, :, 15, 3] = 254
    for g in range(8): F[:, g, 2 * g + 1, 5] = 1
    sel = np.where(rng.random((N, 8, I)) < 0.75, (I - 1) * rng.integers(0, 2, (N, 8, I)), rng.integers(0, I, (N, 8, I)))
    cross = rng.random((N, 8)) < 0.3; cross[0, 0] = False; cross[N - 1, 7] = False; cross[0, 7] = True
    sel[..., 0] = np.where(cross, I - 1, 0); sel[..., I - 1] = np.where(cross, 0, I - 1); sel[..., 1] = 1
    inner = of_class(rng, cl, rng.choice(np.array([0, 1, 1, 1, 2, 2, 2]), (N, 8, L, 16)), 4)
    P = np.where(rng.random((N, 8, L, 16)) < 0.75, np.where(rng.random((N, 8, L, 16)) < rng.random((N, 8, L, 1)), I - 1, 0), inner)
    P[:, :, L - 1] = 1; P[:, :, L - 1, 15] = I - 1; P[:, :, 0] = 1; P[:, :, 0, 8] = I - 1
    P[:, :, L - 2] = 3; P[:, :, L - 2, 12:14] = 0
    P[:, ::2, L - 2, 5] = 2; P[:, ::2, L - 2, 10] = I - 2; P[:, 1::2, L - 2, 5] = I - 2; P[:, 1::2, L - 2, 10] = 2; P[:, :, L - 2, 15] = I - 2
    P[:, :, L - 3] = 4; P[:, :, L - 3, ::3] = I - 3
    P[:, :, L - 4] = 4; P[:, :, L - 4, 3] = 5; P[:, :, L - 4, 15] = 5
    P[::2, :, S] = 4; P[::2, :, S, ::3] = I - 3
    P[1::2, :, S] = 3; P[1::2, :, S, 9] = 2; P[1::2, :, S, 12] = I - 2
    return pack(F, sel, P)
def setup_inputs_corners(rng):
    n = T + 3; hi = rows8(rng); cl = np.argsort(rng.random((N, 8, I)), axis=-1) % n
    u = rng.random((N, 8, 16, I)); c = cl[:, :, None, :]; tall = c == T + 2
    F = np.where(c == 0, 8 * u, np.where(tall == hi, np.where(tall, 208 + 48 * u, 128 + 32 * u), np.where(tall, 8 + 33 * u, 41 * u))).astype(np.int64)
    own = np.arange(I)[None, None, :]; z = rng.integers(0, 3, (N, 8, I)); step = of_class(rng, cl, np.maximum(np.minimum(cl, T) - 1, 0), n)
    sel = np.where(cl == T + 1, own, np.where((cl == 0) | (cl == T + 2), np.where(z == 0, own, np.where(z == 1, 0, I - 1)), step))
    fm = rng.integers(0, 12, (N, 8, 1)); fm[0, 0] = 2; fm[N - 1, 7] = 1; fm[0, 7] = 6; fm[N - 1, 0] = 2; fm[1, 3] = 4; fm[2, 5] = 7
    md = np.where(fm < 6, fm, rng.integers(0, 6, (N, 8, L)))[..., None]
    one = np.arange(16) == rng.integers(0, 16, (N, 8, L, 1)); dd = rng.integers(0, T + 1, (N, 8, L, 1)); mix = rng.integers(0, n, (N, 8, L, 16))
    want = np.where(md == 0, mix, np.where(md == 1, T + 2, np.where(md == 2, np.where(one, T + 2, T + 1), np.where(md == 3, np.where(one, mix, T + 2), np.where(md == 4, np.where(one, T + 2, dd), T + 1)))))
    P = of_class(rng, cl, want, n); P = np.where(md == 1, P[..., :1], P)
    P[:, ::2, 1] = 0; P[:, 1::2, L - 1] = I - 1
    return pack(F, sel, P)
def setup_inputs_ties(rng):
    kind = rng.choice(np.array([0, 1, 1, 2, 2, 3, 4]), (N, 8, I)); rk = np.argsort(rng.random((N, 8, 16, I), dtype=np.float32), axis=2)
    more = np.array([0, 16 - H, 17 - H, 3, 0])[kind][:, :, None, :]; less = np.array([16, 16 - H, 17 - H, 13, 8])[kind][:, :, None, :]
    F = rng.integers(100, 200, (1, 8, 16, 1)) + (rk < more).astype(np.int64) - (rk >= less).astype(np.int64)
    two = rng.permutation(8)[:2]; x = int(rng.integers(0, N))
    for r in (x, (x - 1) % N):
        F[r, two[0]] += 20; F[r, two[1]] += 20
        v = rng.permutation(I)[:I // 16]; F[r, two[1], rng.integers(0, 16, v.size), v] = 0
    return pack(F, rng.integers(0, I, (N, 8, I)), rng.integers(0, I, (N, 8, L, 16)))
def check_inputs(d):
    bad = []
    for k, hi in (("front", 255), ("sel0", I - 1), ("par", I - 1)):
        x = np.asarray(d[k]).astype(np.float64)
        if not (np.min(x) >= 0 and np.max(x) <= hi): bad.append("range of " + k)
        elif np.any(x != np.floor(x)): bad.append("whole numbers in " + k)
    return bad
def reference(front, sel0, par):
    F = np.zeros((N, 8, 16, W), np.int32); F[..., :I] = front.astype(np.float32).reshape(N, 8, 16, I).astype(np.int32)
    sel = np.zeros((N, 8, W), np.int64); sel[..., :I] = sel0
    P = np.stack([gentries(a) for a in par]).astype(np.int64).reshape(N, 8, L, 16)
    i = np.arange(L); k = np.arange(16)
    def fronts(q):
        return np.take_along_axis(F, q.reshape(N, 8, 1, L * 16), 3).reshape(N, 8, 16, L, 16)
    for t in range(R):
        b = I + t * (L + M)
        f = fronts(P); s = np.argmax(np.add.reduce(f, axis=2), axis=3)
        ps = np.take_along_axis(P, s[..., None], 3)[..., 0]; g = np.take_along_axis(F, ps[:, :, None, :], 3)
        q = P; c = np.zeros(P.shape, np.int64); walk = np.ones(P.shape, bool)
        for test in range(T):
            fq = f if test == 0 else fronts(q)
            walk = walk & (np.add.reduce((fq <= g[..., None]).astype(np.int32), axis=2) < H)
            c = c + walk.astype(np.int64)
            q = np.where(walk, np.take_along_axis(sel, q.reshape(N, 8, L * 16), 2).reshape(q.shape), q)
        red = c == T
        new = np.maximum.reduce(fronts(np.where(red, ps[..., None], q)), axis=4)
        new[:, :, (i + t) & 15, i] = np.minimum(255, new[:, :, (i + t) & 15, i] + 1)
        come = np.roll(new[..., ::S], 1 + t % (N - 1), axis=0)
        best = np.argmax(np.add.reduce((f[:, :, :, ::S] <= come[..., None]).astype(np.int32), axis=2), axis=3)
        F[..., b:b + L] = new; F[..., b + L:b + L + M] = come
        sel[..., b:b + L] = ps; sel[..., b + L:b + L + M] = np.take_along_axis(P[:, :, ::S], best[..., None], 3)[..., 0]
        sc = np.add.reduce(c, axis=3)[..., None]; reds = np.add.reduce(red.astype(np.int64), axis=(1, 3))[:, None, :, None]
        P = np.where(k == s[..., None], b + i[:, None], np.where(red, b + ((5 * i[:, None] + 37 * k + sc + reds) & (L - 1)), np.where(c == 0, b + L + ((i[:, None] + k + reds) & (M - 1)), q)))
    return {"yf": np.ascontiguousarray(F[..., I:]).reshape(N, 128, W - I).astype(np.float32).astype(BF), "ys": np.ascontiguousarray(sel[..., I:]).astype(np.float32),
            "yp": np.ascontiguousarray(P.transpose(0, 1, 3, 2)).reshape(N, 128, L).astype(np.float32)}

@@ -1,0 +1,642 @@
+from concourse.mybir import AluOpType, ActivationFunctionType
+
+I0, L, R = 3328, 256, 2
+NB = L + 128
+FW = 4112
+PW = 4160
+BIG = 65536.0
+PR = 8192
+CYC = 1.0e-3
+GAT = 1.56
+WAKE = 0.08
+ORDER = {}
+SUN = [[(4, h, q) for h in (0, 1) for q in range(4)] + [(1, 1, 3)]] * 2
+FQ = ["SSSS", "SSSS"]
+P1Q = ["SSSS", "SSSS"]
+P2Q = ["SSSS", "SSSS"]
+GQ = "VV"
+S2Q = "VS"
+
+SCRATCH = {}
+for _n, _w, _d in [
+        ("F", FW, "bfloat16"), ("PT", PW, "bfloat16"), ("f0", 4096, "bfloat16"), ("f1", 4096, "bfloat16"),
+        ("pa0", 4096, "bfloat16"), ("pa1", 4096, "bfloat16"), ("px", 4096, "bfloat16"),
+        ("cv0", 2048, "bfloat16"), ("cv1", 2048, "bfloat16"), ("cv2", 2048, "bfloat16"), ("cv3", 2048, "bfloat16"),
+        ("cv4", 2048, "bfloat16"), ("cv5", 2048, "bfloat16"), ("fq", 4096, "bfloat16"), ("s2", 3328, "bfloat16"),
+        ("LEa", 144, "bfloat16"), ("LEb", 144, "bfloat16"), ("LEK", 144, "bfloat16"), ("LEC", 144, "bfloat16"),
+        ("ID", 128, "bfloat16"), ("NID", 128, "bfloat16"), ("SU", 128, "bfloat16"),
+        ("SH", 128, "bfloat16"), ("D01", 128, "bfloat16"), ("YSM", 8, "bfloat16"), ("ONES", 128, "bfloat16"),
+        ("KR", 128, "bfloat16"), ("CV", 64, "bfloat16"), ("CS", 64, "bfloat16"),
+        ("PI", 1, "int32"), ("CI", 144, "int32"), ("CU", 128, "int32"), ("CX", 32, "int32"),
+        ("ti", 8, "int32"),
+        ("MA", 256, "int32"), ("MSK0", 256, "bfloat16"), ("MSK1", 256, "bfloat16"),
+        ("K12", 512, "float32"), ("KS0", 256, "float32"), ("KS1", 256, "float32"),
+        ("IDV", 260, "int32"), ("IDW", 260, "int32"), ("IDH", 260, "int32"), ("HB", 260, "bfloat16"),
+        ("LB", 260, "bfloat16"), ("NL", 16, "uint16"), ("NL2", 8, "uint16"), ("NL3", 8, "uint16"), ("XL", 16, "uint16"),
+        ("SELR", 208, "int32"), ("SELP", 208, "int32"), ("SELH", 208, "int32"), ("SELO", 208, "int32"),
+        ("SELL", 208, "uint16"), ("SHB", 208, "bfloat16"), ("SLB", 208, "bfloat16"),
+        ("SHB2", 208, "bfloat16"), ("SLB2", 208, "bfloat16"),
+        ("raw", 256, "int32"), ("PL", 256, "uint16"), ("QLa0", 256, "uint16"), ("QLa1", 256, "uint16"),
+        ("QLb0", 256, "uint16"), ("QLb1", 256, "uint16"), ("LOL0", 128, "uint16"), ("LOL1", 128, "uint16"),
+        ("OFF0", 8, "uint16"), ("OFF1", 8, "uint16"), ("OFFC", 8, "uint16"),
+        ("CO0", 256, "float32"), ("CO1", 256, "float32"), ("CO2", 256, "float32"), ("CO3", 256, "float32"),
+        ("CO4", 256, "float32"), ("ACC", 256, "float32"),
+        ("KEY", 256, "float32"), ("TR", 256, "float32"), ("KC", 128, "float32"), ("MI", 16, "int32"), ("MC", 8, "int32"),
+        ("MN", 24, "int32"), ("G0", 1024, "bfloat16"), ("G1", 1024, "bfloat16"), ("CR", 128, "bfloat16"),
+        ("VI", 256, "int32"), ("HI", 256, "int32"), ("LO", 256, "int32"), ("HIF", 256, "bfloat16"),
+        ("RED", 256, "bfloat16"), ("XA", 32, "float32"),
+        ("E", 256, "float32"), ("XY", 512, "int32"), ("XZ", 512, "int32"), ("T1", 256, "float32"),
+        ("NI", 256, "int32"), ("NUM", 256, "int32"), ("YPR", 256, "float32"),
+        ("DA", 512, "bfloat16"), ("DB", 512, "bfloat16"), ("DC", 512, "bfloat16"), ("DE", 512, "bfloat16"),
+        ("DS", 4096, "bfloat16"),
+        ("NEWP", 256, "bfloat16"), ("NEWN", 256, "bfloat16"), ("SEND0", 128, "bfloat16"), ("SEND1", 128, "bfloat16"),
+        ("PSP", 256, "bfloat16"), ("PSN", 256, "bfloat16"), ("PCP", 128, "bfloat16"), ("PCN", 128, "bfloat16"),
+        ("YS", 768, "float32"), ("cols", 64, "float32")]:
+    SCRATCH[_n] = ("sbuf", [128, _w], _d)
+PSUMS = ["PG0", "PG1", "PCa", "PCb", "PQ0", "PQ1", "PD0", "PD1"]
+for _n in PSUMS:
+    SCRATCH[_n] = ("psum", [128, 512], "float32")
+
+NDMA = 40
+SEMAPHORES = ["sv", "ss", "st", "sg"] + ["d%d" % j for j in range(NDMA)] + ["ar0", "ar1", "lc0", "lc1"]
+
+
+def rank_program(g, core, T, topo):
+    rank = T.rank_of(core)
+    if rank is None:
+        return
+    A = AluOpType
+    AF = ActivationFunctionType
+    ALL = 0xFFFF
+    ops = []
+
+    def X(name, c0, c1, step=1, p=None, rows=ALL):
+        t = T[name]
+        if p is not None:
+            ap = t[0:p, c0:c1]
+        elif step == 1:
+            ap = t[:, c0:c1]
+        else:
+            ap = t[:, c0:c1:step]
+        return (ap, [(name, c0, c1, rows)])
+
+    def ind(win, off):
+        return (win[0].indirect(off[0]), win[1] + off[1], True)
+
+    def rec(kind, q, outs, ins, fn, cost, lat=0.0, data=None):
+        reads = list(dict.fromkeys(r for x in ins for r in x[1]))
+        writes = list(dict.fromkeys(r for x in outs for r in x[1]))
+        ops.append({"kind": kind, "q": q, "r": reads, "w": writes, "fn": fn, "cost": cost, "lat": lat, "data": data})
+
+    def width(x):
+        n = 1
+        for d in x[0].shape[1:]:
+            n *= d
+        return n
+
+    def emit(q, outs, ins, fn, cyc=1.0, gat=False):
+        n = width(outs[0])
+        rec("c", q, outs, ins, fn, 0.06 + n * GAT * CYC if gat else 0.02 + max(64, cyc * n) * CYC)
+
+    def isg(*xs):
+        return any(len(x) > 2 for x in xs)
+
+    def two(*xs):
+        return all(SCRATCH[x[1][0][0]][2] in ("bfloat16", "uint16") for x in xs)
+
+    def vcopy(o, i):
+        emit("V", [o], [i], lambda e: e.tensor_copy(o[0], i[0]), 0.5 if two(o, i) else 1.0, isg(i))
+
+    def vtt(o, a, b, op):
+        cyc = 1.0 if a[1][0][0] in PSUMS or b[1][0][0] in PSUMS else 2.0
+        emit("V", [o], [a, b], lambda e: e.tensor_tensor(o[0], a[0], b[0], op), cyc, isg(a))
+
+    def vts(o, i, s1, op0, s2=None, op1=None):
+        ins = [i] + [s for s in (s1, s2) if isinstance(s, tuple)]
+        a1 = s1[0] if isinstance(s1, tuple) else s1
+        a2 = s2[0] if isinstance(s2, tuple) else s2
+        cyc = 0.5 if two(o, i) else 1.0
+        if op1 is None:
+            emit("V", [o], ins, lambda e: e.tensor_scalar(o[0], i[0], a1, None, op0), cyc)
+        else:
+            emit("V", [o], ins, lambda e: e.tensor_scalar(o[0], i[0], a1, a2, op0, op1), cyc)
+
+    def vset(o, c):
+        emit("V", [o], [], lambda e: e.memset(o[0], c), 0.5 if two(o) else 1.0)
+
+    def act(o, i, func=AF.Copy, bias=0.0, scale=1.0):
+        ins = [i] + [x for x in (bias, scale) if isinstance(x, tuple)]
+        b = bias[0] if isinstance(bias, tuple) else bias
+        s = scale[0] if isinstance(scale, tuple) else scale
+        emit("S", [o], ins, lambda e: e.activation(o[0], i[0], func, bias=b, scale=s), 1.0, isg(i))
+
+    def gather(q, o, i):
+        if q == "V":
+            vcopy(o, i)
+        else:
+            act(o, i)
+
+    def iota(o, pattern, base, cm, fl=False):
+        if fl:
+            emit("G", [o], [], lambda e: e.iota(o[0], pattern, base, cm, allow_small_or_imprecise_dtypes=True), 2.0)
+        else:
+            emit("G", [o], [], lambda e: e.iota(o[0], pattern, base, cm), 2.0)
+
+    def mms(lst):
+        cost = sum(max(64, width(m[2])) for m in lst) * 0.0005
+        rec("t", "T", [m[0] for m in lst], [x for m in lst for x in (m[1], m[2])], None, cost, 0.0, lst)
+
+    def dma(q, outs, ins, pairs, lat=2.3):
+        rec("d", q, outs, ins, None, 0.06 * len(pairs), lat, pairs)
+
+    dma("Y", [X("SELR", 0, 208)], [], [(T.SELR[:], T.sel0[:])])
+    dma("S", [X("F", 16, 16 + I0)], [], [(T.F[:, 16:16 + I0], T.front[:])], 4.8)
+    dma("Y", [X("raw", 0, 256)], [], [(T.raw[:, 16 * k:16 * k + 16], T.par[k::16, :]) for k in range(16)])
+
+    ncol = [0]
+
+    def col():
+        ncol[0] += 1
+        return X("cols", ncol[0] - 1, ncol[0])
+
+    PI, CI, CU = X("PI", 0, 1), X("CI", 0, 128), X("CU", 0, 128)
+    LE = lambda nm, e: X(nm, 15 - e, 143 - e)
+    ti = [X("ti", j, j + 1) for j in range(8)]
+    iota(PI, [[0, 1]], 0, 1)
+    iota(X("CI", 0, 144), [[1, 144]], 0, 0)
+    iota(X("IDV", 0, 260), [[1, 260]], 0, 0)
+    vset(X("PT", 0, PW), 0.0)
+    vset(X("F", 0, 16), 0.0)
+    pf, uf, gf, zf = col(), col(), col(), col()
+    vcopy(pf, PI)
+    vts(ti[0], PI, 15, A.bitwise_and)
+    vts(ti[1], PI, 4, A.arith_shift_right)
+    vcopy(uf, ti[0])
+    vcopy(gf, ti[1])
+    act(zf, gf, AF.Identity, bias=15.0, scale=16.0)
+
+    def split(src, hb, lb):
+        vts(X("SELH", 0, 208), src, 6, A.arith_shift_right)
+        vts(X("SELO", 0, 208), src, 63, A.bitwise_and)
+        vcopy(X(hb, 0, 208), X("SELH", 0, 208))
+        vcopy(X(lb, 0, 208), X("SELO", 0, 208))
+
+    def prow(r, buf, n, c0):
+        o = T.PT[r::16, c0:c0 + 16 * n]
+        dma("Y", [X("PT", c0, c0 + 16 * n, rows=1 << r)], [X(buf, 0, n)], [(o, T[buf][:, 0:n])])
+
+    def wcol(a):
+        o, t = col(), col()
+        vts(o, uf, float(a), A.is_equal, 64.0, A.mult)
+        vts(t, uf, float(a + 1), A.is_equal)
+        vtt(o, o, t, A.add)
+        return o
+
+    SELP = X("SELP", 0, 208)
+    vts(SELP, X("SELR", 0, 208), 16.0, A.add)
+    split(SELP, "SHB", "SLB")
+    prow(2, "SHB", 208, 16)
+    prow(3, "SLB", 208, 16)
+    vcopy(X("SELL", 0, 208), SELP)
+    for h in (0, 1):
+        vts(X("PL", 128 * h, 128 * h + 128), X("raw", h, 256, 2), 16.0, A.add)
+    u260 = col()
+    act(u260, uf, scale=260.0)
+    vts(X("IDW", 0, 260), X("IDV", 0, 260), u260, A.add)
+    vts(X("IDH", 0, 260), X("IDW", 0, 260), 6, A.arith_shift_right)
+    vcopy(X("HB", 0, 260), X("IDH", 0, 260))
+    vts(X("IDV", 0, 260), X("IDW", 0, 260), 63, A.bitwise_and)
+    vcopy(X("LB", 0, 260), X("IDV", 0, 260))
+    swin = X("PT", 0, 16 + I0)
+    gather(S2Q[0], X("s2", 0, 1664), ind(swin, X("SELL", 0, 104)))
+    gather(S2Q[1], X("s2", 1664, 3328), ind(swin, X("SELL", 104, 208)))
+    wa = wcol(2)
+    vts(X("LEa", 0, 144), X("CI", 0, 144), zf, A.is_equal, wa, A.mult)
+    mms([(X("PQ0", 0, 208), LE("LEa", e), X("s2", e, 3328, 16), e == 0, e == 15) for e in range(16)])
+    vcopy(SELP, X("PQ0", 0, 208))
+    split(SELP, "SHB2", "SLB2")
+    prow(4, "SHB2", 208, 16)
+    prow(5, "SLB2", 208, 16)
+    prow(0, "HB", 260, 0)
+    prow(1, "LB", 260, 0)
+    wb = wcol(4)
+    for nm, wt in (("LEb", wb), ("LEK", 4096.0), ("LEC", BIG)):
+        vts(X(nm, 0, 144), X("CI", 0, 144), zf, A.is_equal, wt, A.mult)
+    vset(X("ONES", 0, 128), 1.0)
+    vts(X("KR", 0, 128), CI, -0.125, A.mult, 15.875, A.add)
+    u2032 = col()
+    act(u2032, uf, AF.Identity, bias=2032.0)
+    ID, NID = X("ID", 0, 128), X("NID", 0, 128)
+    vts(ID, CI, pf, A.is_equal)
+    act(NID, ID, scale=-1.0)
+    vset(X("CV", 0, 64), -10.0 * BIG / 128)
+    vset(X("CS", 0, 64), -4.0 * BIG / 128)
+    for h in (0, 1):
+        vts(X("CO0", 128 * h, 128 * h + 128), X("raw", h, 256, 2), 16.0 + 5 * PR, A.add)
+    vts(CU, CI, 15, A.bitwise_and)
+    vts(X("SU", 0, 128), CU, uf, A.is_equal)
+    l4, p3, l2 = col(), col(), col()
+    vts(l4, uf, 4.0, A.is_lt)
+    vts(p3, pf, 3.0, A.add)
+    vtt(p3, p3, l4, A.mult)
+    vts(p3, p3, -1.0, A.add)
+    vts(X("SH", 0, 128), CI, p3, A.is_equal)
+    vts(l2, uf, 2.0, A.is_lt)
+    act(X("D01", 0, 128), ID, scale=l2)
+    w01 = wcol(0)
+    vts(X("YSM", 0, 8), X("CI", 0, 8), gf, A.is_equal, w01, A.mult)
+    na, nb, nc, c7, b3, u8 = col(), col(), col(), col(), col(), col()
+    vts(ti[2], PI, 1, A.bitwise_and)
+    vts(ti[3], PI, 1, A.arith_shift_right, 7, A.bitwise_and)
+    vts(ti[4], PI, 7, A.bitwise_and)
+    vts(ti[5], PI, 3, A.arith_shift_right, 1, A.bitwise_and)
+    vts(na, ti[2], 128.0, A.mult)
+    vts(nb, ti[3], 16.0, A.mult)
+    vtt(na, na, nb, A.add)
+    vts(X("NL", 0, 16), X("CI", 0, 16), na, A.add)
+    act(u8, uf, scale=8.0)
+    vts(X("NL2", 0, 8), X("CI", 0, 8), u8, A.add)
+    vcopy(c7, ti[4])
+    vts(b3, c7, 16.0, A.mult)
+    vcopy(nc, ti[5])
+    vtt(b3, b3, nc, A.add)
+    vts(X("NL3", 0, 8), X("CI", 0, 8), 2.0, A.mult, b3, A.add)
+    vts(X("CX", 0, 16), X("CI", 0, 16), 3, A.arith_shift_right)
+    vts(X("XL", 0, 16), X("CX", 0, 16), 8.0, A.mult, c7, A.add)
+    iota(X("MA", 0, 256), [[1, 256]], 128, -1)
+    vts(X("MA", 0, 256), X("MA", 0, 256), 15, A.bitwise_and)
+    vts(X("MSK0", 0, 256), X("MA", 0, 256), 0.0, A.is_equal)
+    vts(X("MSK1", 0, 256), X("MA", 0, 256), 15.0, A.is_equal)
+    u80, u16 = col(), col()
+    act(u80, uf, scale=80.0)
+    act(u16, uf, scale=16.0)
+    for h in (0, 1):
+        iota(X("K12", 256 * h, 256 * h + 128), [[37, 16], [10, 8]], 80 + 5 * h, 0, True)
+        iota(X("K12", 256 * h + 128, 256 * h + 256), [[1, 16], [2, 8]], h, 0, True)
+        for j, ub in ((0, u80), (128, u16)):
+            kx = X("K12", 256 * h + j, 256 * h + j + 128)
+            act(kx, kx, AF.Identity, bias=ub)
+    for t in range(R):
+        ks = X("KS%d" % t, 0, 256)
+        iota(ks, [[1, 2], [0, 16], [2, 8]], 8 * PR + I0 + NB * t + 16, 0, True)
+        act(ks, ks, AF.Identity, bias=u16)
+
+    def sumto(bank, o0, n, le, src, s0, const=None):
+        o = X(bank, o0, o0 + n)
+        l = []
+        if const is not None:
+            l.append((o, X("ONES", 0, 128), const, True, False))
+        for e in range(16):
+            l.append((o, LE(le, e), X(src, s0 + e, s0 + 16 * n, 16), e == 0 and const is None, e == 15))
+        mms(l)
+
+    def tree(z, src, s0, out, o0, bank, off):
+        r = 128 * (z & 1)
+        vcopy(X(src, s0, s0 + 128), X(bank, 0, 128))
+        vtt(X("TR", r, r + 64), X(src, s0, s0 + 64), X(src, s0 + 64, s0 + 128), A.max)
+        vtt(X("TR", r + 64, r + 96), X("TR", r, r + 32), X("TR", r + 32, r + 64), A.max)
+        vtt(X("TR", r + 96, r + 112), X("TR", r + 64, r + 80), X("TR", r + 80, r + 96), A.max)
+        vtt(X(out, o0, o0 + 8), X("TR", r + 96, r + 104), X("TR", r + 104, r + 112), A.max)
+        vts(X("MN", 8 * z, 8 * z + 8), X(out, o0, o0 + 8), 4095, A.bitwise_and)
+        vts(X(off, 0, 8), X("MN", 8 * z, 8 * z + 8), -1.0, A.mult, u2032, A.add)
+
+    def grow(src, n, c0, y0, tt, bank):
+        yo = 256 if n == 256 else 384
+        y = X(bank, yo, yo + n, p=8)
+        if tt + 1 < R:
+            mms([(X(bank, 0, n), X("SH", 0, 128), X(src, 0, n), True, False),
+                 (X(bank, 0, n), X("D01", 0, 128), X("PT", c0, c0 + n), False, True)])
+            act(X("PT", c0, c0 + n), X(bank, 0, n))
+        mms([(y, X("YSM", 0, 8), X(src, 0, n), True, True)])
+        act(X("YS", y0, y0 + n, p=8), y, AF.Identity, bias=-16.0)
+        dma("Y", [], [X("YS", y0, y0 + n, p=8)], [(T.ys[:, y0:y0 + n], T.YS[0:8, y0:y0 + n])])
+
+    def come(tt):
+        cc = 16 + I0 + NB * tt + L
+        ft, pt = "f%d" % tt, "pa%d" % tt
+        vcopy(X("CR", 0, 128), ind(X("F", cc, cc + 128), X("NL2", 0, 8)))
+        mms([(X("PD0", 128 * j, 128 * j + 128), ID, X("CR", 0, 128), True, True) for j in range(4)])
+        for j in range(4):
+            vtt(X("cv0", 512 * j, 512 * j + 512), X(ft, 512 * j, 512 * j + 512), X("PD0", 0, 512), A.is_le)
+            if j & 1:
+                sumto("PCa", 32 * (j - 1), 64, "LEK", "cv0", 512 * (j - 1), X("KR", 32 * (j - 1), 32 * (j - 1) + 64))
+        tree(2, "KC", 0, "MC", 0, "PCa", "OFFC")
+        act(X("PCP", 0, 128), ind(X(pt, 0, 2048), X("OFFC", 0, 8)))
+        act(X("PCN", 0, 128), ind(X("PCP", 0, 128), X("NL3", 0, 8)))
+        grow("PCN", 128, cc, NB * tt + L, tt, "PCb")
+
+    for t in range(R):
+        B = I0 + NB * t
+        cc = 16 + B + L
+        fn, pn = "f%d" % t, "pa%d" % t
+        win = X("F", 0, 16 + B)
+        pwin = X("PT", 0, 16 + B)
+        KB = ("PCa", "PCb")
+        for h in (0, 1):
+            for ch in (0, 1):
+                c0 = 128 * h + 64 * ch
+                gather(FQ[t][2 * h + ch], X(fn, 16 * c0, 16 * c0 + 1024), ind(win, X("PL", c0, c0 + 64)))
+                sumto(KB[h], 64 * ch, 64, "LEK", fn, 16 * c0, X("KR", 64 * ch, 64 * ch + 64))
+        for h in (0, 1):
+            tree(h, "KEY", 128 * h, "MI", 8 * h, KB[h], "OFF%d" % h)
+            vcopy(X("G%d" % h, 0, 128), ind(X(fn, 2048 * h, 2048 * h + 2048), X("OFF%d" % h, 0, 8)))
+            mms([(X("PG%d" % h, 128 * j, 128 * j + 128), ID, X("G%d" % h, 0, 128), True, True) for j in range(4)])
+        for h in (0, 1):
+            for n in (128, 256, 512):
+                gather(GQ[t], X("G%d" % h, n, 2 * n), X("G%d" % h, 0, n))
+            for j in range(4):
+                s0 = 2048 * h + 512 * j
+                o = X("cv%d" % h, 512 * j, 512 * j + 512)
+                if (0, h, j) in SUN[t]:
+                    pd = X("PD%d" % (j & 1), 0, 512)
+                    mms([(pd, NID, X(fn, s0, s0 + 512), True, False), (pd, ID, X("G%d" % h, 0, 512), False, True)])
+                    act(o, pd, AF.Sign, bias=0.5)
+                else:
+                    vtt(o, X(fn, s0, s0 + 512), X("PG%d" % h, 0, 512), A.is_le)
+                sumto(KB[h], 32 * j, 32, "LEC", "cv%d" % h, 512 * j, X("CS" if (0, h, j) in SUN[t] else "CV", 0, 32))
+
+        def comb(d, h, bank):
+            hs = (128 * h, 128 * h + 128)
+            acc = X("ACC", *hs)
+            if d == 0:
+                vtt(acc, X(bank, 0, 128), X("CO0", *hs), A.min)
+                act(acc, acc, AF.Relu)
+            else:
+                vtt(X(bank, 128, 256), X(bank, 0, 128), X("CO%d" % d, *hs), A.min)
+                vtt(X("VI", *hs) if d == 4 else acc, X(bank, 128, 256), acc, A.max)
+
+        comb(0, 0, "PCa")
+        comb(0, 1, "PCb")
+
+        def path(h, dst, lst, nm, d0, qs):
+            for ch in (0, 1):
+                s0 = 2048 * h + 1024 * ch
+                gather(qs[2 * h + ch], X(dst, s0, s0 + 1024), ind(pwin, lst(ch)))
+                for d, le in ((0, "LEa"), (1, "LEb")):
+                    sumto("PQ%d" % h, 128 * d + 64 * ch, 64, le, dst, s0)
+            vcopy(X("%s%d" % (nm, h), 0, 256), X("PQ%d" % h, 0, 256))
+            for j in (0, 1):
+                act(X("CO%d" % (d0 + j), 128 * h, 128 * h + 128), X("PQ%d" % h, 128 * j, 128 * j + 128), AF.Identity,
+                    bias=float(PR * (5 - d0 - j)))
+
+        for h in (0, 1):
+            path(h, pn, lambda ch: X("PL", 128 * h + 64 * ch, 128 * h + 64 * ch + 64), "QLa", 1, P1Q[t])
+        for h in (0, 1):
+            path(h, "px", lambda ch: X("QLa%d" % h, 128 + 64 * ch, 192 + 64 * ch), "QLb", 3, P2Q[t])
+
+        banks = {(1, 0): "PCa", (1, 1): "PCb", (2, 0): "PCa", (2, 1): "PCb", (3, 0): "PG0", (3, 1): "PG1",
+                 (4, 0): "PQ0", (4, 1): "PQ1"}
+        ns = [0]
+        for n, (d, h) in enumerate([(d, h) for d in (1, 2, 3, 4) for h in (0, 1)]):
+            nm, o = ("QLa%d" % h, 128 * (d - 1)) if d < 3 else ("QLb%d" % h, 128 * (d - 3))
+            buf = "cv%d" % ((n + 2) % 6)
+            bank = banks[(d, h)]
+            for j in (0, 2):
+                two_s = [(d, h, j + i) in SUN[t] for i in (0, 1)]
+                if not any(two_s):
+                    vtt(X(buf, 512 * j, 512 * j + 1024), ind(win, X(nm, o + 32 * j, o + 32 * j + 64)),
+                        X("G%d" % h, 0, 1024), A.is_le)
+                for i in (0, 1):
+                    s0, o1 = 512 * (j + i), o + 32 * (j + i)
+                    if two_s[i]:
+                        q = ns[0] % 8
+                        ns[0] += 1
+                        pd = X("PD%d" % (q & 1), 0, 512)
+                        fq = X("fq", 512 * q, 512 * q + 512)
+                        act(fq, ind(win, X(nm, o1, o1 + 32)))
+                        mms([(pd, NID, fq, True, False), (pd, ID, X("G%d" % h, 0, 512), False, True)])
+                        act(X(buf, s0, s0 + 512), pd, AF.Sign, bias=0.5)
+                    elif any(two_s):
+                        vtt(X(buf, s0, s0 + 512), ind(win, X(nm, o1, o1 + 32)), X("G%d" % h, 0, 512), A.is_le)
+                if two_s[0] == two_s[1]:
+                    sumto(bank, 32 * j, 64, "LEC", buf, 512 * j, X("CS" if two_s[0] else "CV", 0, 64))
+                else:
+                    for i in (0, 1):
+                        sumto(bank, 32 * (j + i), 32, "LEC", buf, 512 * (j + i), X("CS" if two_s[i] else "CV", 0, 32))
+            comb(d, h, bank)
+
+        for h in (0, 1):
+            hs = (128 * h, 128 * h + 128)
+            vts(X("LO", *hs), X("VI", *hs), PR - 1, A.bitwise_and)
+            vcopy(X("LOL%d" % h, 0, 128), X("LO", *hs))
+            ll = "LOL%d" % h
+            db = ("PD0", "PD1", "PCa", "PCb")
+            ds = [X("DS", 2048 * h + 512 * j, 2048 * h + 512 * j + 512) for j in range(4)]
+            for j in range(4):
+                if j == 3 and h == 0:
+                    vcopy(ds[3], ind(win, X(ll, 96, 128)))
+                else:
+                    act(ds[j], ind(win, X(ll, 32 * j, 32 * j + 32)))
+            for j in range(3):
+                bank = db[(3 * h + j) % 4]
+                jj = j + h
+                mms([(X(bank, 0, 512), ID, ds[jj], True, True)])
+                prev, nx = (ds[3] if h == 0 else ds[0]) if j == 0 else X(("DA", "DB")[j - 1], 0, 512), ("DA", "DB", "DC")[j]
+                if j < 2:
+                    vtt(X(nx, 0, 512), X(bank, 0, 512), prev, A.max)
+            vtt(X("DC", 0, 256), X(bank, 0, 256), X("DB", 0, 256), A.max)
+            vtt(X(bank, 256, 512), X(bank, 256, 512), X("DB", 256, 512), A.max)
+            vtt(X("DE", 0, 128), X(bank, 256, 384), X("DC", 0, 128), A.max)
+            vtt(X(bank, 0, 128), X(bank, 384, 512), X("DC", 128, 256), A.max)
+            vtt(X("NEWP", 128 * h, 128 * h + 128), X(bank, 0, 128), X("DE", 0, 128), A.max)
+        vtt(X("NEWN", 0, 256), ind(X("NEWP", 0, 256), X("NL", 0, 16)), X("MSK%d" % t, 0, 256), A.add)
+        vts(X("SEND%d" % t, 0, 128), X("NEWN", 0, 256, 2), 255.0, A.min)
+        dst = T.cores[(rank + 1 + t % 7) % len(T.cores)]
+        src = T.cores[(rank - 1 - t % 7) % len(T.cores)]
+        es = topo.engines(core, dst)[:8]
+        nsrc = len(topo.engines(src, core)[:8])
+        rid, pid, _se = topo.addr(dst)
+        mk = sum(1 << e for e in es)
+
+        def send(e, t=t, cc=cc, rid=rid, pid=pid, mk=mk):
+            e.remote_dma(out_ap=T.F[:, cc:cc + 128], in_ap=T["SEND%d" % t][:], remote_sem=T.sem["ar%d" % t],
+                         local_sem=T.sem["lc%d" % t], pid=pid, routing_id=rid, dma_engine_mask=mk)
+
+        rec("s", "G", [], [X("SEND%d" % t, 0, 128)], send, 0.3, 2.0, ("lc%d" % t, len(es)))
+        rec("a", "R", [X("F", cc, cc + 128)], [X("SEND%d" % t, 0, 128)], None, 0.3, 2.0, ("ar%d" % t, nsrc))
+        vts(X("F", 16 + B, 16 + B + L), X("NEWN", 0, 256), 255.0, A.min)
+        if t + 1 == R:
+            come(t)
+        kr, kc = float(7 * PR + B + 16), float(6 * PR + B + L + 16)
+        for h in (0, 1):
+            hs = (128 * h, 128 * h + 128)
+            hif, red = X("HIF", *hs), X("RED", *hs)
+            pq, pg = "PQ%d" % h, "PG%d" % h
+            vts(X("HI", *hs), X("VI", *hs), 13, A.arith_shift_right)
+            vcopy(hif, X("HI", *hs))
+            act(red, hif, AF.Relu, bias=1.0, scale=-1.0)
+            act(X(pq, 0, 128), hif, AF.Relu, bias=kr, scale=-kr)
+            act(X(pq, 128, 256), hif, AF.Relu, bias=-4.0 * kc, scale=kc)
+            kk = [(128 * h + 8 * k, 128 * h + 8 * k + 8) for k in range(16)]
+            o1, o2 = X(pg, 0, 8), X(pg, 8, 16)
+            mms([(o1, NID, X("HIF", *c), n == 0, False) for n, c in enumerate(kk)]
+                + [(o1, X("SU", 0, 128), X("RED", *c), False, n == 15) for n, c in enumerate(kk)]
+                + [(o2, X("SU", 0, 128), X("RED", *c), n == 0, n == 15) for n, c in enumerate(kk)])
+            e = X("E", *hs)
+            vtt(e, ind(X("MI", 8 * h, 8 * h + 8), X("XL", 0, 8)), X("KEY", *hs), A.is_equal)
+            vtt(X(pq, 384, 512), e, X("KS%d" % t, *hs), A.mult)
+            xa = X("XA", 16 * h, 16 * h + 16)
+            vcopy(xa, X(pg, 0, 16))
+            q0 = 256 * h
+            vtt(X("XY", q0, q0 + 256), ind(xa, X("XL", 0, 16)), X("K12", q0, q0 + 256), A.add)
+            vts(X("XZ", q0, q0 + 128), X("XY", q0, q0 + 128), 255, A.bitwise_and)
+            vts(X("XZ", q0 + 128, q0 + 256), X("XY", q0 + 128, q0 + 256), 127, A.bitwise_and)
+            t1 = X("T1", *hs)
+            vtt(X(pq, 256, 384), X(pq, 0, 128), X("XZ", q0, q0 + 128), A.add)
+            vtt(t1, X(pq, 128, 256), X("XZ", q0 + 128, q0 + 256), A.add)
+            vtt(t1, X(pq, 256, 384), t1, A.max)
+            vtt(X(pq, 384, 512), X(pq, 384, 512), X("VI", *hs), A.max)
+            vtt(X("NI", *hs), X(pq, 384, 512), t1, A.max)
+            vts(X("NUM", *hs), X("NI", *hs), PR - 1, A.bitwise_and)
+            if t + 1 < R:
+                vcopy(X("PL", *hs), X("NUM", *hs))
+                vts(X("CO0", *hs), X("NUM", *hs), float(5 * PR), A.add)
+            else:
+                vts(X("YPR", h, 256, 2), X("NUM", *hs), -16.0, A.add)
+        if t + 1 == R:
+            dma("Y", [], [X("YPR", 0, 256)], [(T.yp[k::16, :], T.YPR[:, 16 * k:16 * k + 16]) for k in range(16)])
+        for h in (0, 1):
+            act(X("PSP", 128 * h, 128 * h + 128), ind(X(pn, 2048 * h, 2048 * h + 2048), X("OFF%d" % h, 0, 8)))
+        act(X("PSN", 0, 256), ind(X("PSP", 0, 256), X("NL", 0, 16)))
+        grow("PSN", 256, 16 + B, NB * t, t, "PD1")
+        y0 = NB * t
+        dma("Y", [], [X("F", 16 + B, 16 + B + L)], [(T.yf[:, y0:y0 + L], T.F[:, 16 + B:16 + B + L])])
+        dma("Y", [], [X("F", cc, cc + 128)], [(T.yf[:, y0 + L:y0 + NB], T.F[:, cc:cc + 128])])
+        if t + 1 < R:
+            come(t)
+
+    def schedule():
+        n = len(ops)
+        pred = [set() for _ in range(n)]
+        last = {}
+        for i, o in enumerate(ops):
+            for w, regs in ((0, o["r"]), (1, o["w"])):
+                for (b, c0, c1, rows) in regs:
+                    l = last.setdefault(b, [])
+                    ps = b in PSUMS
+                    for (j, w2, d0, d1, r2) in l:
+                        if j != i and ((ps and ops[j]["q"] != o["q"]) or ((w or w2) and d0 < c1 and c0 < d1 and (rows & r2))):
+                            pred[i].add(j)
+                    if w and not ps:
+                        l[:] = [x for x in l if not (x[2] >= c0 and x[3] <= c1 and (x[4] & ~rows) == 0)]
+                    l.append((i, w, c0, c1, rows))
+        succ = [[] for _ in range(n)]
+        for i in range(n):
+            for j in pred[i]:
+                succ[j].append(i)
+        prio = [0.0] * n
+        for i in range(n - 1, -1, -1):
+            prio[i] = ops[i]["cost"] + ops[i]["lat"] + max([prio[k] + WAKE for k in succ[i]] or [0.0])
+        left = [len(p) for p in pred]
+        ready = {}
+        fin = [0.0] * n
+        free = {}
+        est = [0.0] * n
+        for i in range(n):
+            if not left[i]:
+                ready.setdefault(ops[i]["q"], []).append(i)
+        order = []
+        while len(order) < n:
+            best = None
+            for q, l in ready.items():
+                if not l:
+                    continue
+                f = free.get(q, 0.0)
+                t0 = min(max(f, est[i]) for i in l)
+                i = max((x for x in l if max(f, est[x]) <= t0 + 0.03), key=lambda x: prio[x])
+                st = max(f, est[i])
+                if best is None or st < best[0]:
+                    best = (st, i, q)
+            st, i, q = best
+            ready[q].remove(i)
+            order.append(i)
+            free[q] = st + ops[i]["cost"]
+            fin[i] = free[q] + ops[i]["lat"]
+            for k in succ[i]:
+                est[k] = max(est[k], fin[i] + WAKE)
+                left[k] -= 1
+                if not left[k]:
+                    ready.setdefault(ops[k]["q"], []).append(k)
+        return order
+
+    eng = {"V": g.vector, "S": g.scalar, "T": g.tensor, "G": g, "Y": g.sync}
+    sname = {"V": "sv", "S": "ss", "T": "st", "G": "sg"}
+    cnt = {"V": 0, "S": 0, "T": 0, "G": 0}
+    clk = {q: {} for q in "VSTGY"}
+    log = {}
+    total = {}
+    ndma = [0]
+
+    def waits(q, reads, writes):
+        need = []
+        for w, regs in ((0, reads), (1, writes)):
+            for (b, c0, c1, rows) in regs:
+                ps = b in PSUMS
+                for e in log.get(b, []):
+                    if ps and e["q"] != q:
+                        need.append(e)
+                        continue
+                    if (ps and q == "T") or not (e["w"] or w) or e["c1"] <= c0 or e["c0"] >= c1 or not (e["rows"] & rows):
+                        continue
+                    if e["q"] == q and w and not e["w"]:
+                        continue
+                    need.append(e)
+        want = {}
+        for e in need:
+            if clk[q].get(e["sem"], 0) < e["val"] and want.get(e["sem"], (0, None))[0] < e["val"]:
+                want[e["sem"]] = (e["val"], e)
+        for s in list(want):
+            v = want[s][0]
+            for s2 in want:
+                if s2 != s and want[s2][1]["clk"].get(s, 0) >= v:
+                    del want[s]
+                    break
+        for s, (v, e) in want.items():
+            eng[q].wait_ge(T.sem[s], v)
+            for a, b in e["clk"].items():
+                clk[q][a] = max(clk[q].get(a, 0), b)
+            clk[q][s] = max(clk[q].get(s, 0), v)
+
+    def note(q, reads, writes, sem, val, c):
+        c = dict(c)
+        c[sem] = max(c.get(sem, 0), val)
+        total[sem] = max(total.get(sem, 0), val)
+        for w, regs in ((0, reads), (1, writes)):
+            for (b, c0, c1, rows) in regs:
+                l = log.setdefault(b, [])
+                if b in PSUMS:
+                    l[:] = [e for e in l if not (e["q"] == q and e["c0"] >= c0 and e["c1"] <= c1 and (w or not e["w"]))]
+                elif w:
+                    l[:] = [e for e in l if not (e["c0"] >= c0 and e["c1"] <= c1 and (e["rows"] & ~rows) == 0)]
+                l.append({"q": q, "w": w, "c0": c0, "c1": c1, "rows": rows, "sem": sem, "val": val, "clk": c})
+
+    if "order" not in ORDER:
+        ORDER["order"] = schedule()
+    for i in ORDER["order"]:
+        o = ops[i]
+        q, r, w = o["q"], o["r"], o["w"]
+        if o["kind"] == "a":
+            note("D", [], w, o["data"][0], o["data"][1], {})
+            continue
+        waits(q, r, w)
+        if o["kind"] == "c":
+            cnt[q] += 1
+            o["fn"](eng[q]).then_inc(T.sem[sname[q]], 1)
+            note(q, r, w, sname[q], cnt[q], clk[q])
+        elif o["kind"] == "t":
+            for (x, lh, rh, a, b) in o["data"]:
+                cnt["T"] += 1
+                g.tensor.matmul(x[0], lh[0], rh[0], a, b).then_inc(T.sem.st, 1)
+            note("T", r, w, "st", cnt["T"], clk["T"])
+        elif o["kind"] == "d":
+            sem = "d%d" % ndma[0]
+            ndma[0] += 1
+            for (x, y) in o["data"]:
+                eng[q].dma_start(x, y).then_inc(T.sem[sem], 16)
+            note("D", r, w, sem, 16 * len(o["data"]), clk[q])
+        else:
+            o["fn"](g)
+            note("D", r, w, o["data"][0], o["data"][1], clk["G"])
+    for s, v in total.items():
+        if clk["Y"].get(s, 0) < v:
+            g.sync.wait_ge(T.sem[s], v)

@@ -10,11 +10,16 @@ CYC = 1.0e-3
 GAT = 1.56
 WAKE = 0.08
 ORDER = {}
-SUN = [[(4, h, q) for h in (0, 1) for q in range(4)] + [(1, 1, 3)]] * 2
-FQ = ["SSSS", "SSSS"]
+SUN = [[(0, 1, 0), (0, 1, 1), (0, 1, 3), (2, 1, 2), (3, 1, 0), (3, 1, 1), (4, 0, 0), (4, 0, 1), (4, 0, 2), (4, 0, 3),
+        (4, 1, 0), (4, 1, 1)],
+       [(0, 0, 0), (0, 0, 1), (2, 1, 2), (3, 1, 2), (3, 1, 3), (4, 0, 0), (4, 0, 1), (4, 0, 2), (4, 0, 3), (4, 1, 2),
+        (4, 1, 3)]]
+FQ = ["SSSS", "SVSS"]
 P1Q = ["SSSS", "SSSS"]
 P2Q = ["SSSS", "SSSS"]
-GQ = "VV"
+GQ = ["VV", "VV"]
+CQ = "VS"
+DV = ["VS", "VS"]
 S2Q = "VS"
 
 SCRATCH = {}
@@ -22,8 +27,8 @@ for _n, _w, _d in [
         ("F", FW, "bfloat16"), ("PT", PW, "bfloat16"), ("f0", 4096, "bfloat16"), ("f1", 4096, "bfloat16"),
         ("pa0", 4096, "bfloat16"), ("pa1", 4096, "bfloat16"), ("px", 4096, "bfloat16"),
         ("cv0", 2048, "bfloat16"), ("cv1", 2048, "bfloat16"), ("cv2", 2048, "bfloat16"), ("cv3", 2048, "bfloat16"),
-        ("cv4", 2048, "bfloat16"), ("cv5", 2048, "bfloat16"), ("fq", 4096, "bfloat16"), ("s2", 3328, "bfloat16"),
-        ("LEa", 144, "bfloat16"), ("LEb", 144, "bfloat16"), ("LEK", 144, "bfloat16"), ("LEC", 144, "bfloat16"),
+        ("cv4", 2048, "bfloat16"), ("cvc", 2048, "bfloat16"), ("cv5", 2048, "bfloat16"), ("fq", 4096, "bfloat16"), ("s2", 3328, "bfloat16"),
+        ("LEH", 144, "bfloat16"), ("LEa", 144, "bfloat16"), ("LEb", 144, "bfloat16"), ("LEK", 144, "bfloat16"), ("LEC", 144, "bfloat16"),
         ("ID", 128, "bfloat16"), ("NID", 128, "bfloat16"), ("SU", 128, "bfloat16"),
         ("SH", 128, "bfloat16"), ("D01", 128, "bfloat16"), ("YSM", 8, "bfloat16"), ("ONES", 128, "bfloat16"),
         ("KR", 128, "bfloat16"), ("CV", 64, "bfloat16"), ("CS", 64, "bfloat16"),
@@ -165,7 +170,8 @@ def rank_program(g, core, T, topo):
     iota(PI, [[0, 1]], 0, 1)
     iota(X("CI", 0, 144), [[1, 144]], 0, 0)
     iota(X("IDV", 0, 260), [[1, 260]], 0, 0)
-    vset(X("PT", 0, PW), 0.0)
+    vset(X("PT", 0, PW // 2), 0.0)
+    act(X("PT", PW // 2, PW), X("PT", 0, PW // 2))
     vset(X("F", 0, 16), 0.0)
     pf, uf, gf, zf = col(), col(), col(), col()
     vcopy(pf, PI)
@@ -220,7 +226,7 @@ def rank_program(g, core, T, topo):
     prow(0, "HB", 260, 0)
     prow(1, "LB", 260, 0)
     wb = wcol(4)
-    for nm, wt in (("LEb", wb), ("LEK", 4096.0), ("LEC", BIG)):
+    for nm, wt in (("LEb", wb), ("LEK", 4096.0), ("LEC", BIG), ("LEH", 2048.0)):
         vts(X(nm, 0, 144), X("CI", 0, 144), zf, A.is_equal, wt, A.mult)
     vset(X("ONES", 0, 128), 1.0)
     vts(X("KR", 0, 128), CI, -0.125, A.mult, 15.875, A.add)
@@ -315,15 +321,28 @@ def rank_program(g, core, T, topo):
         cc = 16 + I0 + NB * tt + L
         ft, pt = "f%d" % tt, "pa%d" % tt
         vcopy(X("CR", 0, 128), ind(X("F", cc, cc + 128), X("NL2", 0, 8)))
-        mms([(X("PD0", 128 * j, 128 * j + 128), ID, X("CR", 0, 128), True, True) for j in range(4)])
+        cr, onS = X("CR", 0, 128), CQ[tt] == "S"
+        kb = "PQ1" if onS else "PD0"
+        if not onS:
+            mms([(X("PQ1", 128 * j, 128 * j + 128), ID, cr, True, True) for j in range(4)])
         for j in range(4):
-            vtt(X("cv0", 512 * j, 512 * j + 512), X(ft, 512 * j, 512 * j + 512), X("PD0", 0, 512), A.is_le)
+            fj, cj, pd = X(ft, 512 * j, 512 * j + 512), X("cvc", 512 * j, 512 * j + 512), "PD%d" % (j & 1)
+            if onS:
+                l = []
+                for i in range(4):
+                    o = X(pd, 128 * i, 128 * i + 128)
+                    l += [(o, ID, cr, True, False), (o, NID, X(ft, 512 * j + 128 * i, 512 * j + 128 * i + 128), False, True)]
+                mms(l)
+                act(cj, X(pd, 0, 512), AF.Sign, bias=0.5)
+            else:
+                vtt(cj, fj, X("PQ1", 0, 512), A.is_le)
             if j & 1:
-                sumto("PCa", 32 * (j - 1), 64, "LEK", "cv0", 512 * (j - 1), X("KR", 32 * (j - 1), 32 * (j - 1) + 64))
-        tree(2, "KC", 0, "MC", 0, "PCa", "OFFC")
+                sumto(kb, 32 * (j - 1), 64, "LEH" if onS else "LEK", "cvc", 512 * (j - 1),
+                      X("KR", 32 * (j - 1), 32 * (j - 1) + 64))
+        tree(2, "KC", 0, "MC", 0, kb, "OFFC")
         act(X("PCP", 0, 128), ind(X(pt, 0, 2048), X("OFFC", 0, 8)))
         act(X("PCN", 0, 128), ind(X("PCP", 0, 128), X("NL3", 0, 8)))
-        grow("PCN", 128, cc, NB * tt + L, tt, "PCb")
+        grow("PCN", 128, cc, NB * tt + L, tt, "PD1")
 
     for t in range(R):
         B = I0 + NB * t
@@ -343,7 +362,7 @@ def rank_program(g, core, T, topo):
             mms([(X("PG%d" % h, 128 * j, 128 * j + 128), ID, X("G%d" % h, 0, 128), True, True) for j in range(4)])
         for h in (0, 1):
             for n in (128, 256, 512):
-                gather(GQ[t], X("G%d" % h, n, 2 * n), X("G%d" % h, 0, n))
+                gather(GQ[t][h], X("G%d" % h, n, 2 * n), X("G%d" % h, 0, n))
             for j in range(4):
                 s0 = 2048 * h + 512 * j
                 o = X("cv%d" % h, 512 * j, 512 * j + 512)
@@ -353,7 +372,13 @@ def rank_program(g, core, T, topo):
                     act(o, pd, AF.Sign, bias=0.5)
                 else:
                     vtt(o, X(fn, s0, s0 + 512), X("PG%d" % h, 0, 512), A.is_le)
-                sumto(KB[h], 32 * j, 32, "LEC", "cv%d" % h, 512 * j, X("CS" if (0, h, j) in SUN[t] else "CV", 0, 32))
+                sg = [(0, h, i) in SUN[t] for i in (j - 1, j)]
+                if j & 1 and sg[0] == sg[1]:
+                    sumto(KB[h], 32 * (j - 1), 64, "LEC", "cv%d" % h, 512 * (j - 1), X("CS" if sg[1] else "CV", 0, 64))
+                elif j & 1:
+                    for i in (0, 1):
+                        sumto(KB[h], 32 * (j - 1 + i), 32, "LEC", "cv%d" % h, 512 * (j - 1 + i),
+                              X("CS" if sg[i] else "CV", 0, 32))
 
         def comb(d, h, bank):
             hs = (128 * h, 128 * h + 128)
@@ -384,13 +409,12 @@ def rank_program(g, core, T, topo):
         for h in (0, 1):
             path(h, "px", lambda ch: X("QLa%d" % h, 128 + 64 * ch, 192 + 64 * ch), "QLb", 3, P2Q[t])
 
-        banks = {(1, 0): "PCa", (1, 1): "PCb", (2, 0): "PCa", (2, 1): "PCb", (3, 0): "PG0", (3, 1): "PG1",
-                 (4, 0): "PQ0", (4, 1): "PQ1"}
         ns = [0]
-        for n, (d, h) in enumerate([(d, h) for d in (1, 2, 3, 4) for h in (0, 1)]):
+
+        def test(d, h):
             nm, o = ("QLa%d" % h, 128 * (d - 1)) if d < 3 else ("QLb%d" % h, 128 * (d - 3))
-            buf = "cv%d" % ((n + 2) % 6)
-            bank = banks[(d, h)]
+            buf = "cv%d" % ((4 * h + d + 1) % 6)
+            bank = (("PCa", "PCb"), ("PG0", "PG1"))[h][d & 1]
             for j in (0, 2):
                 two_s = [(d, h, j + i) in SUN[t] for i in (0, 1)]
                 if not any(two_s):
@@ -415,23 +439,23 @@ def rank_program(g, core, T, topo):
                         sumto(bank, 32 * (j + i), 32, "LEC", buf, 512 * (j + i), X("CS" if two_s[i] else "CV", 0, 32))
             comb(d, h, bank)
 
-        for h in (0, 1):
+        def largest(h):
             hs = (128 * h, 128 * h + 128)
             vts(X("LO", *hs), X("VI", *hs), PR - 1, A.bitwise_and)
             vcopy(X("LOL%d" % h, 0, 128), X("LO", *hs))
             ll = "LOL%d" % h
-            db = ("PD0", "PD1", "PCa", "PCb")
+            db = ("PCa", "PCb")
             ds = [X("DS", 2048 * h + 512 * j, 2048 * h + 512 * j + 512) for j in range(4)]
             for j in range(4):
-                if j == 3 and h == 0:
+                if j == 3 and DV[t][h] == "V":
                     vcopy(ds[3], ind(win, X(ll, 96, 128)))
                 else:
                     act(ds[j], ind(win, X(ll, 32 * j, 32 * j + 32)))
             for j in range(3):
-                bank = db[(3 * h + j) % 4]
-                jj = j + h
+                bank = db[(h + j) % 2]
+                jj = j + (DV[t][h] == "S")
                 mms([(X(bank, 0, 512), ID, ds[jj], True, True)])
-                prev, nx = (ds[3] if h == 0 else ds[0]) if j == 0 else X(("DA", "DB")[j - 1], 0, 512), ("DA", "DB", "DC")[j]
+                prev, nx = (ds[3] if DV[t][h] == "V" else ds[0]) if j == 0 else X(("DA", "DB")[j - 1], 0, 512), ("DA", "DB", "DC")[j]
                 if j < 2:
                     vtt(X(nx, 0, 512), X(bank, 0, 512), prev, A.max)
             vtt(X("DC", 0, 256), X(bank, 0, 256), X("DB", 0, 256), A.max)
@@ -439,8 +463,15 @@ def rank_program(g, core, T, topo):
             vtt(X("DE", 0, 128), X(bank, 256, 384), X("DC", 0, 128), A.max)
             vtt(X(bank, 0, 128), X(bank, 384, 512), X("DC", 128, 256), A.max)
             vtt(X("NEWP", 128 * h, 128 * h + 128), X(bank, 0, 128), X("DE", 0, 128), A.max)
-        vtt(X("NEWN", 0, 256), ind(X("NEWP", 0, 256), X("NL", 0, 16)), X("MSK%d" % t, 0, 256), A.add)
-        vts(X("SEND%d" % t, 0, 128), X("NEWN", 0, 256, 2), 255.0, A.min)
+            nw = X("NEWN", 128 * h, 128 * h + 128)
+            vtt(nw, ind(X("NEWP", 128 * h, 128 * h + 128), X("NL3", 0, 8)), X("MSK%d" % t, h, 256, 2), A.add)
+            if h == 0:
+                vts(X("SEND%d" % t, 0, 128), nw, 255.0, A.min)
+            vts(X("F", 16 + B + h, 16 + B + L, 2), nw, 255.0, A.min)
+
+        for d in (1, 2, 3, 4):
+            test(d, 0)
+        largest(0)
         dst = T.cores[(rank + 1 + t % 7) % len(T.cores)]
         src = T.cores[(rank - 1 - t % 7) % len(T.cores)]
         es = topo.engines(core, dst)[:8]
@@ -454,21 +485,23 @@ def rank_program(g, core, T, topo):
 
         rec("s", "G", [], [X("SEND%d" % t, 0, 128)], send, 0.3, 2.0, ("lc%d" % t, len(es)))
         rec("a", "R", [X("F", cc, cc + 128)], [X("SEND%d" % t, 0, 128)], None, 0.3, 2.0, ("ar%d" % t, nsrc))
-        vts(X("F", 16 + B, 16 + B + L), X("NEWN", 0, 256), 255.0, A.min)
+        for d in (1, 2, 3, 4):
+            test(d, 1)
         if t + 1 == R:
             come(t)
+        largest(1)
         kr, kc = float(7 * PR + B + 16), float(6 * PR + B + L + 16)
         for h in (0, 1):
             hs = (128 * h, 128 * h + 128)
             hif, red = X("HIF", *hs), X("RED", *hs)
-            pq, pg = "PQ%d" % h, "PG%d" % h
+            pq = ("PQ0", "PG0")[h]
             vts(X("HI", *hs), X("VI", *hs), 13, A.arith_shift_right)
             vcopy(hif, X("HI", *hs))
             act(red, hif, AF.Relu, bias=1.0, scale=-1.0)
             act(X(pq, 0, 128), hif, AF.Relu, bias=kr, scale=-kr)
             act(X(pq, 128, 256), hif, AF.Relu, bias=-4.0 * kc, scale=kc)
             kk = [(128 * h + 8 * k, 128 * h + 8 * k + 8) for k in range(16)]
-            o1, o2 = X(pg, 0, 8), X(pg, 8, 16)
+            o1, o2 = X(pq, 256, 264), X(pq, 264, 272)
             mms([(o1, NID, X("HIF", *c), n == 0, False) for n, c in enumerate(kk)]
                 + [(o1, X("SU", 0, 128), X("RED", *c), False, n == 15) for n, c in enumerate(kk)]
                 + [(o2, X("SU", 0, 128), X("RED", *c), n == 0, n == 15) for n, c in enumerate(kk)])
@@ -476,7 +509,7 @@ def rank_program(g, core, T, topo):
             vtt(e, ind(X("MI", 8 * h, 8 * h + 8), X("XL", 0, 8)), X("KEY", *hs), A.is_equal)
             vtt(X(pq, 384, 512), e, X("KS%d" % t, *hs), A.mult)
             xa = X("XA", 16 * h, 16 * h + 16)
-            vcopy(xa, X(pg, 0, 16))
+            vcopy(xa, X(pq, 256, 272))
             q0 = 256 * h
             vtt(X("XY", q0, q0 + 256), ind(xa, X("XL", 0, 16)), X("K12", q0, q0 + 256), A.add)
             vts(X("XZ", q0, q0 + 128), X("XY", q0, q0 + 128), 255, A.bitwise_and)
@@ -498,7 +531,7 @@ def rank_program(g, core, T, topo):
         for h in (0, 1):
             act(X("PSP", 128 * h, 128 * h + 128), ind(X(pn, 2048 * h, 2048 * h + 2048), X("OFF%d" % h, 0, 8)))
         act(X("PSN", 0, 256), ind(X("PSP", 0, 256), X("NL", 0, 16)))
-        grow("PSN", 256, 16 + B, NB * t, t, "PD1")
+        grow("PSN", 256, 16 + B, NB * t, t, "PG1")
         y0 = NB * t
         dma("Y", [], [X("F", 16 + B, 16 + B + L)], [(T.yf[:, y0:y0 + L], T.F[:, 16 + B:16 + B + L])])
         dma("Y", [], [X("F", cc, cc + 128)], [(T.yf[:, y0 + L:y0 + NB], T.F[:, cc:cc + 128])])

from concourse.mybir import AluOpType, ActivationFunctionType

I0, L, R = 3328, 256, 2
NB = L + 128
FW = 4112
PW = 4160
BIG = 65536.0
PR = 8192
CYC = 1.0e-3
GAT = 1.56
WAKE = 0.08
ORDER = {}
SUN = [[(0, 1, 0), (0, 1, 1), (0, 1, 3), (2, 1, 2), (3, 1, 0), (3, 1, 1), (4, 0, 0), (4, 0, 1), (4, 0, 2), (4, 0, 3),
        (4, 1, 0), (4, 1, 1)],
       [(0, 0, 0), (0, 0, 1), (2, 1, 2), (3, 1, 2), (3, 1, 3), (4, 0, 0), (4, 0, 1), (4, 0, 2), (4, 0, 3), (4, 1, 2),
        (4, 1, 3)]]
FQ = ["SSSS", "SVSS"]
P1Q = ["SSSS", "SSSS"]
P2Q = ["SSSS", "SSSS"]
GQ = ["VV", "VV"]
CQ = "VS"
DV = ["VS", "VS"]
S2Q = "VS"

SCRATCH = {}
for _n, _w, _d in [
        ("F", FW, "bfloat16"), ("PT", PW, "bfloat16"), ("f0", 4096, "bfloat16"), ("f1", 4096, "bfloat16"),
        ("pa0", 4096, "bfloat16"), ("pa1", 4096, "bfloat16"), ("px", 4096, "bfloat16"),
        ("cv0", 2048, "bfloat16"), ("cv1", 2048, "bfloat16"), ("cv2", 2048, "bfloat16"), ("cv3", 2048, "bfloat16"),
        ("cv4", 2048, "bfloat16"), ("cvc", 2048, "bfloat16"), ("cv5", 2048, "bfloat16"), ("fq", 4096, "bfloat16"), ("s2", 3328, "bfloat16"),
        ("LEH", 144, "bfloat16"), ("LEa", 144, "bfloat16"), ("LEb", 144, "bfloat16"), ("LEK", 144, "bfloat16"), ("LEC", 144, "bfloat16"),
        ("ID", 128, "bfloat16"), ("NID", 128, "bfloat16"), ("SU", 128, "bfloat16"),
        ("SH", 128, "bfloat16"), ("D01", 128, "bfloat16"), ("YSM", 8, "bfloat16"), ("ONES", 128, "bfloat16"),
        ("KR", 128, "bfloat16"), ("CV", 64, "bfloat16"), ("CS", 64, "bfloat16"),
        ("PI", 1, "int32"), ("CI", 144, "int32"), ("CU", 128, "int32"), ("CX", 32, "int32"),
        ("ti", 8, "int32"),
        ("MA", 256, "int32"), ("MSK0", 256, "bfloat16"), ("MSK1", 256, "bfloat16"),
        ("K12", 512, "float32"), ("KS0", 256, "float32"), ("KS1", 256, "float32"),
        ("IDV", 260, "int32"), ("IDW", 260, "int32"), ("IDH", 260, "int32"), ("HB", 260, "bfloat16"),
        ("LB", 260, "bfloat16"), ("NL", 16, "uint16"), ("NL2", 8, "uint16"), ("NL3", 8, "uint16"), ("XL", 16, "uint16"),
        ("SELR", 208, "int32"), ("SELP", 208, "int32"), ("SELH", 208, "int32"), ("SELO", 208, "int32"),
        ("SELL", 208, "uint16"), ("SHB", 208, "bfloat16"), ("SLB", 208, "bfloat16"),
        ("SHB2", 208, "bfloat16"), ("SLB2", 208, "bfloat16"),
        ("raw", 256, "int32"), ("PL", 256, "uint16"), ("QLa0", 256, "uint16"), ("QLa1", 256, "uint16"),
        ("QLb0", 256, "uint16"), ("QLb1", 256, "uint16"), ("LOL0", 128, "uint16"), ("LOL1", 128, "uint16"),
        ("OFF0", 8, "uint16"), ("OFF1", 8, "uint16"), ("OFFC", 8, "uint16"),
        ("CO0", 256, "float32"), ("CO1", 256, "float32"), ("CO2", 256, "float32"), ("CO3", 256, "float32"),
        ("CO4", 256, "float32"), ("ACC", 256, "float32"),
        ("KEY", 256, "float32"), ("TR", 256, "float32"), ("KC", 128, "float32"), ("MI", 16, "int32"), ("MC", 8, "int32"),
        ("MN", 24, "int32"), ("G0", 1024, "bfloat16"), ("G1", 1024, "bfloat16"), ("CR", 128, "bfloat16"),
        ("VI", 256, "int32"), ("HI", 256, "int32"), ("LO", 256, "int32"), ("HIF", 256, "bfloat16"),
        ("RED", 256, "bfloat16"), ("XA", 32, "float32"),
        ("E", 256, "float32"), ("XY", 512, "int32"), ("XZ", 512, "int32"), ("T1", 256, "float32"),
        ("NI", 256, "int32"), ("NUM", 256, "int32"), ("YPR", 256, "float32"),
        ("DA", 512, "bfloat16"), ("DB", 512, "bfloat16"), ("DC", 512, "bfloat16"), ("DE", 512, "bfloat16"),
        ("DS", 4096, "bfloat16"),
        ("NEWP", 256, "bfloat16"), ("NEWN", 256, "bfloat16"), ("SEND0", 128, "bfloat16"), ("SEND1", 128, "bfloat16"),
        ("PSP", 256, "bfloat16"), ("PSN", 256, "bfloat16"), ("PCP", 128, "bfloat16"), ("PCN", 128, "bfloat16"),
        ("YS", 768, "float32"), ("cols", 64, "float32")]:
    SCRATCH[_n] = ("sbuf", [128, _w], _d)
PSUMS = ["PG0", "PG1", "PCa", "PCb", "PQ0", "PQ1", "PD0", "PD1"]
for _n in PSUMS:
    SCRATCH[_n] = ("psum", [128, 512], "float32")

NDMA = 40
SEMAPHORES = ["sv", "ss", "st", "sg"] + ["d%d" % j for j in range(NDMA)] + ["ar0", "ar1", "lc0", "lc1"]


def rank_program(g, core, T, topo):
    rank = T.rank_of(core)
    if rank is None:
        return
    A = AluOpType
    AF = ActivationFunctionType
    ALL = 0xFFFF
    ops = []

    def X(name, c0, c1, step=1, p=None, rows=ALL):
        t = T[name]
        if p is not None:
            ap = t[0:p, c0:c1]
        elif step == 1:
            ap = t[:, c0:c1]
        else:
            ap = t[:, c0:c1:step]
        return (ap, [(name, c0, c1, rows)])

    def ind(win, off):
        return (win[0].indirect(off[0]), win[1] + off[1], True)

    def rec(kind, q, outs, ins, fn, cost, lat=0.0, data=None):
        reads = list(dict.fromkeys(r for x in ins for r in x[1]))
        writes = list(dict.fromkeys(r for x in outs for r in x[1]))
        ops.append({"kind": kind, "q": q, "r": reads, "w": writes, "fn": fn, "cost": cost, "lat": lat, "data": data})

    def width(x):
        n = 1
        for d in x[0].shape[1:]:
            n *= d
        return n

    def emit(q, outs, ins, fn, cyc=1.0, gat=False):
        n = width(outs[0])
        rec("c", q, outs, ins, fn, 0.06 + n * GAT * CYC if gat else 0.02 + max(64, cyc * n) * CYC)

    def isg(*xs):
        return any(len(x) > 2 for x in xs)

    def two(*xs):
        return all(SCRATCH[x[1][0][0]][2] in ("bfloat16", "uint16") for x in xs)

    def vcopy(o, i):
        emit("V", [o], [i], lambda e: e.tensor_copy(o[0], i[0]), 0.5 if two(o, i) else 1.0, isg(i))

    def vtt(o, a, b, op):
        cyc = 1.0 if a[1][0][0] in PSUMS or b[1][0][0] in PSUMS else 2.0
        emit("V", [o], [a, b], lambda e: e.tensor_tensor(o[0], a[0], b[0], op), cyc, isg(a))

    def vts(o, i, s1, op0, s2=None, op1=None):
        ins = [i] + [s for s in (s1, s2) if isinstance(s, tuple)]
        a1 = s1[0] if isinstance(s1, tuple) else s1
        a2 = s2[0] if isinstance(s2, tuple) else s2
        cyc = 0.5 if two(o, i) else 1.0
        if op1 is None:
            emit("V", [o], ins, lambda e: e.tensor_scalar(o[0], i[0], a1, None, op0), cyc)
        else:
            emit("V", [o], ins, lambda e: e.tensor_scalar(o[0], i[0], a1, a2, op0, op1), cyc)

    def vset(o, c):
        emit("V", [o], [], lambda e: e.memset(o[0], c), 0.5 if two(o) else 1.0)

    def act(o, i, func=AF.Copy, bias=0.0, scale=1.0):
        ins = [i] + [x for x in (bias, scale) if isinstance(x, tuple)]
        b = bias[0] if isinstance(bias, tuple) else bias
        s = scale[0] if isinstance(scale, tuple) else scale
        emit("S", [o], ins, lambda e: e.activation(o[0], i[0], func, bias=b, scale=s), 1.0, isg(i))

    def gather(q, o, i):
        if q == "V":
            vcopy(o, i)
        else:
            act(o, i)

    def iota(o, pattern, base, cm, fl=False):
        if fl:
            emit("G", [o], [], lambda e: e.iota(o[0], pattern, base, cm, allow_small_or_imprecise_dtypes=True), 2.0)
        else:
            emit("G", [o], [], lambda e: e.iota(o[0], pattern, base, cm), 2.0)

    def mms(lst):
        cost = sum(max(64, width(m[2])) for m in lst) * 0.0005
        rec("t", "T", [m[0] for m in lst], [x for m in lst for x in (m[1], m[2])], None, cost, 0.0, lst)

    def dma(q, outs, ins, pairs, lat=2.3):
        rec("d", q, outs, ins, None, 0.06 * len(pairs), lat, pairs)

    dma("Y", [X("SELR", 0, 208)], [], [(T.SELR[:], T.sel0[:])])
    dma("S", [X("F", 16, 16 + I0)], [], [(T.F[:, 16:16 + I0], T.front[:])], 4.8)
    dma("Y", [X("raw", 0, 256)], [], [(T.raw[:, 16 * k:16 * k + 16], T.par[k::16, :]) for k in range(16)])

    ncol = [0]

    def col():
        ncol[0] += 1
        return X("cols", ncol[0] - 1, ncol[0])

    PI, CI, CU = X("PI", 0, 1), X("CI", 0, 128), X("CU", 0, 128)
    LE = lambda nm, e: X(nm, 15 - e, 143 - e)
    ti = [X("ti", j, j + 1) for j in range(8)]
    iota(PI, [[0, 1]], 0, 1)
    iota(X("CI", 0, 144), [[1, 144]], 0, 0)
    iota(X("IDV", 0, 260), [[1, 260]], 0, 0)
    vset(X("PT", 0, PW // 2), 0.0)
    act(X("PT", PW // 2, PW), X("PT", 0, PW // 2))
    vset(X("F", 0, 16), 0.0)
    pf, uf, gf, zf = col(), col(), col(), col()
    vcopy(pf, PI)
    vts(ti[0], PI, 15, A.bitwise_and)
    vts(ti[1], PI, 4, A.arith_shift_right)
    vcopy(uf, ti[0])
    vcopy(gf, ti[1])
    act(zf, gf, AF.Identity, bias=15.0, scale=16.0)

    def split(src, hb, lb):
        vts(X("SELH", 0, 208), src, 6, A.arith_shift_right)
        vts(X("SELO", 0, 208), src, 63, A.bitwise_and)
        vcopy(X(hb, 0, 208), X("SELH", 0, 208))
        vcopy(X(lb, 0, 208), X("SELO", 0, 208))

    def prow(r, buf, n, c0):
        o = T.PT[r::16, c0:c0 + 16 * n]
        dma("Y", [X("PT", c0, c0 + 16 * n, rows=1 << r)], [X(buf, 0, n)], [(o, T[buf][:, 0:n])])

    def wcol(a):
        o, t = col(), col()
        vts(o, uf, float(a), A.is_equal, 64.0, A.mult)
        vts(t, uf, float(a + 1), A.is_equal)
        vtt(o, o, t, A.add)
        return o

    SELP = X("SELP", 0, 208)
    vts(SELP, X("SELR", 0, 208), 16.0, A.add)
    split(SELP, "SHB", "SLB")
    prow(2, "SHB", 208, 16)
    prow(3, "SLB", 208, 16)
    vcopy(X("SELL", 0, 208), SELP)
    for h in (0, 1):
        vts(X("PL", 128 * h, 128 * h + 128), X("raw", h, 256, 2), 16.0, A.add)
    u260 = col()
    act(u260, uf, scale=260.0)
    vts(X("IDW", 0, 260), X("IDV", 0, 260), u260, A.add)
    vts(X("IDH", 0, 260), X("IDW", 0, 260), 6, A.arith_shift_right)
    vcopy(X("HB", 0, 260), X("IDH", 0, 260))
    vts(X("IDV", 0, 260), X("IDW", 0, 260), 63, A.bitwise_and)
    vcopy(X("LB", 0, 260), X("IDV", 0, 260))
    swin = X("PT", 0, 16 + I0)
    gather(S2Q[0], X("s2", 0, 1664), ind(swin, X("SELL", 0, 104)))
    gather(S2Q[1], X("s2", 1664, 3328), ind(swin, X("SELL", 104, 208)))
    wa = wcol(2)
    vts(X("LEa", 0, 144), X("CI", 0, 144), zf, A.is_equal, wa, A.mult)
    mms([(X("PQ0", 0, 208), LE("LEa", e), X("s2", e, 3328, 16), e == 0, e == 15) for e in range(16)])
    vcopy(SELP, X("PQ0", 0, 208))
    split(SELP, "SHB2", "SLB2")
    prow(4, "SHB2", 208, 16)
    prow(5, "SLB2", 208, 16)
    prow(0, "HB", 260, 0)
    prow(1, "LB", 260, 0)
    wb = wcol(4)
    for nm, wt in (("LEb", wb), ("LEK", 4096.0), ("LEC", BIG), ("LEH", 2048.0)):
        vts(X(nm, 0, 144), X("CI", 0, 144), zf, A.is_equal, wt, A.mult)
    vset(X("ONES", 0, 128), 1.0)
    vts(X("KR", 0, 128), CI, -0.125, A.mult, 15.875, A.add)
    u2032 = col()
    act(u2032, uf, AF.Identity, bias=2032.0)
    ID, NID = X("ID", 0, 128), X("NID", 0, 128)
    vts(ID, CI, pf, A.is_equal)
    act(NID, ID, scale=-1.0)
    vset(X("CV", 0, 64), -10.0 * BIG / 128)
    vset(X("CS", 0, 64), -4.0 * BIG / 128)
    for h in (0, 1):
        vts(X("CO0", 128 * h, 128 * h + 128), X("raw", h, 256, 2), 16.0 + 5 * PR, A.add)
    vts(CU, CI, 15, A.bitwise_and)
    vts(X("SU", 0, 128), CU, uf, A.is_equal)
    l4, p3, l2 = col(), col(), col()
    vts(l4, uf, 4.0, A.is_lt)
    vts(p3, pf, 3.0, A.add)
    vtt(p3, p3, l4, A.mult)
    vts(p3, p3, -1.0, A.add)
    vts(X("SH", 0, 128), CI, p3, A.is_equal)
    vts(l2, uf, 2.0, A.is_lt)
    act(X("D01", 0, 128), ID, scale=l2)
    w01 = wcol(0)
    vts(X("YSM", 0, 8), X("CI", 0, 8), gf, A.is_equal, w01, A.mult)
    na, nb, nc, c7, b3, u8 = col(), col(), col(), col(), col(), col()
    vts(ti[2], PI, 1, A.bitwise_and)
    vts(ti[3], PI, 1, A.arith_shift_right, 7, A.bitwise_and)
    vts(ti[4], PI, 7, A.bitwise_and)
    vts(ti[5], PI, 3, A.arith_shift_right, 1, A.bitwise_and)
    vts(na, ti[2], 128.0, A.mult)
    vts(nb, ti[3], 16.0, A.mult)
    vtt(na, na, nb, A.add)
    vts(X("NL", 0, 16), X("CI", 0, 16), na, A.add)
    act(u8, uf, scale=8.0)
    vts(X("NL2", 0, 8), X("CI", 0, 8), u8, A.add)
    vcopy(c7, ti[4])
    vts(b3, c7, 16.0, A.mult)
    vcopy(nc, ti[5])
    vtt(b3, b3, nc, A.add)
    vts(X("NL3", 0, 8), X("CI", 0, 8), 2.0, A.mult, b3, A.add)
    vts(X("CX", 0, 16), X("CI", 0, 16), 3, A.arith_shift_right)
    vts(X("XL", 0, 16), X("CX", 0, 16), 8.0, A.mult, c7, A.add)
    iota(X("MA", 0, 256), [[1, 256]], 128, -1)
    vts(X("MA", 0, 256), X("MA", 0, 256), 15, A.bitwise_and)
    vts(X("MSK0", 0, 256), X("MA", 0, 256), 0.0, A.is_equal)
    vts(X("MSK1", 0, 256), X("MA", 0, 256), 15.0, A.is_equal)
    u80, u16 = col(), col()
    act(u80, uf, scale=80.0)
    act(u16, uf, scale=16.0)
    for h in (0, 1):
        iota(X("K12", 256 * h, 256 * h + 128), [[37, 16], [10, 8]], 80 + 5 * h, 0, True)
        iota(X("K12", 256 * h + 128, 256 * h + 256), [[1, 16], [2, 8]], h, 0, True)
        for j, ub in ((0, u80), (128, u16)):
            kx = X("K12", 256 * h + j, 256 * h + j + 128)
            act(kx, kx, AF.Identity, bias=ub)
    for t in range(R):
        ks = X("KS%d" % t, 0, 256)
        iota(ks, [[1, 2], [0, 16], [2, 8]], 8 * PR + I0 + NB * t + 16, 0, True)
        act(ks, ks, AF.Identity, bias=u16)

    def sumto(bank, o0, n, le, src, s0, const=None):
        o = X(bank, o0, o0 + n)
        l = []
        if const is not None:
            l.append((o, X("ONES", 0, 128), const, True, False))
        for e in range(16):
            l.append((o, LE(le, e), X(src, s0 + e, s0 + 16 * n, 16), e == 0 and const is None, e == 15))
        mms(l)

    def tree(z, src, s0, out, o0, bank, off):
        r = 128 * (z & 1)
        vcopy(X(src, s0, s0 + 128), X(bank, 0, 128))
        vtt(X("TR", r, r + 64), X(src, s0, s0 + 64), X(src, s0 + 64, s0 + 128), A.max)
        vtt(X("TR", r + 64, r + 96), X("TR", r, r + 32), X("TR", r + 32, r + 64), A.max)
        vtt(X("TR", r + 96, r + 112), X("TR", r + 64, r + 80), X("TR", r + 80, r + 96), A.max)
        vtt(X(out, o0, o0 + 8), X("TR", r + 96, r + 104), X("TR", r + 104, r + 112), A.max)
        vts(X("MN", 8 * z, 8 * z + 8), X(out, o0, o0 + 8), 4095, A.bitwise_and)
        vts(X(off, 0, 8), X("MN", 8 * z, 8 * z + 8), -1.0, A.mult, u2032, A.add)

    def grow(src, n, c0, y0, tt, bank):
        yo = 256 if n == 256 else 384
        y = X(bank, yo, yo + n, p=8)
        if tt + 1 < R:
            mms([(X(bank, 0, n), X("SH", 0, 128), X(src, 0, n), True, False),
                 (X(bank, 0, n), X("D01", 0, 128), X("PT", c0, c0 + n), False, True)])
            act(X("PT", c0, c0 + n), X(bank, 0, n))
        mms([(y, X("YSM", 0, 8), X(src, 0, n), True, True)])
        act(X("YS", y0, y0 + n, p=8), y, AF.Identity, bias=-16.0)
        dma("Y", [], [X("YS", y0, y0 + n, p=8)], [(T.ys[:, y0:y0 + n], T.YS[0:8, y0:y0 + n])])

    def come(tt):
        cc = 16 + I0 + NB * tt + L
        ft, pt = "f%d" % tt, "pa%d" % tt
        vcopy(X("CR", 0, 128), ind(X("F", cc, cc + 128), X("NL2", 0, 8)))
        cr, onS = X("CR", 0, 128), CQ[tt] == "S"
        kb = "PQ1" if onS else "PD0"
        if not onS:
            mms([(X("PQ1", 128 * j, 128 * j + 128), ID, cr, True, True) for j in range(4)])
        for j in range(4):
            fj, cj, pd = X(ft, 512 * j, 512 * j + 512), X("cvc", 512 * j, 512 * j + 512), "PD%d" % (j & 1)
            if onS:
                l = []
                for i in range(4):
                    o = X(pd, 128 * i, 128 * i + 128)
                    l += [(o, ID, cr, True, False), (o, NID, X(ft, 512 * j + 128 * i, 512 * j + 128 * i + 128), False, True)]
                mms(l)
                act(cj, X(pd, 0, 512), AF.Sign, bias=0.5)
            else:
                vtt(cj, fj, X("PQ1", 0, 512), A.is_le)
            if j & 1:
                sumto(kb, 32 * (j - 1), 64, "LEH" if onS else "LEK", "cvc", 512 * (j - 1),
                      X("KR", 32 * (j - 1), 32 * (j - 1) + 64))
        tree(2, "KC", 0, "MC", 0, kb, "OFFC")
        act(X("PCP", 0, 128), ind(X(pt, 0, 2048), X("OFFC", 0, 8)))
        act(X("PCN", 0, 128), ind(X("PCP", 0, 128), X("NL3", 0, 8)))
        grow("PCN", 128, cc, NB * tt + L, tt, "PD1")

    for t in range(R):
        B = I0 + NB * t
        cc = 16 + B + L
        fn, pn = "f%d" % t, "pa%d" % t
        win = X("F", 0, 16 + B)
        pwin = X("PT", 0, 16 + B)
        KB = ("PCa", "PCb")
        for h in (0, 1):
            for ch in (0, 1):
                c0 = 128 * h + 64 * ch
                gather(FQ[t][2 * h + ch], X(fn, 16 * c0, 16 * c0 + 1024), ind(win, X("PL", c0, c0 + 64)))
                sumto(KB[h], 64 * ch, 64, "LEK", fn, 16 * c0, X("KR", 64 * ch, 64 * ch + 64))
        for h in (0, 1):
            tree(h, "KEY", 128 * h, "MI", 8 * h, KB[h], "OFF%d" % h)
            vcopy(X("G%d" % h, 0, 128), ind(X(fn, 2048 * h, 2048 * h + 2048), X("OFF%d" % h, 0, 8)))
            mms([(X("PG%d" % h, 128 * j, 128 * j + 128), ID, X("G%d" % h, 0, 128), True, True) for j in range(4)])
        for h in (0, 1):
            for n in (128, 256, 512):
                gather(GQ[t][h], X("G%d" % h, n, 2 * n), X("G%d" % h, 0, n))
            for j in range(4):
                s0 = 2048 * h + 512 * j
                o = X("cv%d" % h, 512 * j, 512 * j + 512)
                if (0, h, j) in SUN[t]:
                    pd = X("PD%d" % (j & 1), 0, 512)
                    mms([(pd, NID, X(fn, s0, s0 + 512), True, False), (pd, ID, X("G%d" % h, 0, 512), False, True)])
                    act(o, pd, AF.Sign, bias=0.5)
                else:
                    vtt(o, X(fn, s0, s0 + 512), X("PG%d" % h, 0, 512), A.is_le)
                sg = [(0, h, i) in SUN[t] for i in (j - 1, j)]
                if j & 1 and sg[0] == sg[1]:
                    sumto(KB[h], 32 * (j - 1), 64, "LEC", "cv%d" % h, 512 * (j - 1), X("CS" if sg[1] else "CV", 0, 64))
                elif j & 1:
                    for i in (0, 1):
                        sumto(KB[h], 32 * (j - 1 + i), 32, "LEC", "cv%d" % h, 512 * (j - 1 + i),
                              X("CS" if sg[i] else "CV", 0, 32))

        def comb(d, h, bank):
            hs = (128 * h, 128 * h + 128)
            acc = X("ACC", *hs)
            if d == 0:
                vtt(acc, X(bank, 0, 128), X("CO0", *hs), A.min)
                act(acc, acc, AF.Relu)
            else:
                vtt(X(bank, 128, 256), X(bank, 0, 128), X("CO%d" % d, *hs), A.min)
                vtt(X("VI", *hs) if d == 4 else acc, X(bank, 128, 256), acc, A.max)

        comb(0, 0, "PCa")
        comb(0, 1, "PCb")

        def path(h, dst, lst, nm, d0, qs):
            for ch in (0, 1):
                s0 = 2048 * h + 1024 * ch
                gather(qs[2 * h + ch], X(dst, s0, s0 + 1024), ind(pwin, lst(ch)))
                for d, le in ((0, "LEa"), (1, "LEb")):
                    sumto("PQ%d" % h, 128 * d + 64 * ch, 64, le, dst, s0)
            vcopy(X("%s%d" % (nm, h), 0, 256), X("PQ%d" % h, 0, 256))
            for j in (0, 1):
                act(X("CO%d" % (d0 + j), 128 * h, 128 * h + 128), X("PQ%d" % h, 128 * j, 128 * j + 128), AF.Identity,
                    bias=float(PR * (5 - d0 - j)))

        for h in (0, 1):
            path(h, pn, lambda ch: X("PL", 128 * h + 64 * ch, 128 * h + 64 * ch + 64), "QLa", 1, P1Q[t])
        for h in (0, 1):
            path(h, "px", lambda ch: X("QLa%d" % h, 128 + 64 * ch, 192 + 64 * ch), "QLb", 3, P2Q[t])

        ns = [0]

        def test(d, h):
            nm, o = ("QLa%d" % h, 128 * (d - 1)) if d < 3 else ("QLb%d" % h, 128 * (d - 3))
            buf = "cv%d" % ((4 * h + d + 1) % 6)
            bank = (("PCa", "PCb"), ("PG0", "PG1"))[h][d & 1]
            for j in (0, 2):
                two_s = [(d, h, j + i) in SUN[t] for i in (0, 1)]
                if not any(two_s):
                    vtt(X(buf, 512 * j, 512 * j + 1024), ind(win, X(nm, o + 32 * j, o + 32 * j + 64)),
                        X("G%d" % h, 0, 1024), A.is_le)
                for i in (0, 1):
                    s0, o1 = 512 * (j + i), o + 32 * (j + i)
                    if two_s[i]:
                        q = ns[0] % 8
                        ns[0] += 1
                        pd = X("PD%d" % (q & 1), 0, 512)
                        fq = X("fq", 512 * q, 512 * q + 512)
                        act(fq, ind(win, X(nm, o1, o1 + 32)))
                        mms([(pd, NID, fq, True, False), (pd, ID, X("G%d" % h, 0, 512), False, True)])
                        act(X(buf, s0, s0 + 512), pd, AF.Sign, bias=0.5)
                    elif any(two_s):
                        vtt(X(buf, s0, s0 + 512), ind(win, X(nm, o1, o1 + 32)), X("G%d" % h, 0, 512), A.is_le)
                if two_s[0] == two_s[1]:
                    sumto(bank, 32 * j, 64, "LEC", buf, 512 * j, X("CS" if two_s[0] else "CV", 0, 64))
                else:
                    for i in (0, 1):
                        sumto(bank, 32 * (j + i), 32, "LEC", buf, 512 * (j + i), X("CS" if two_s[i] else "CV", 0, 32))
            comb(d, h, bank)

        def largest(h):
            hs = (128 * h, 128 * h + 128)
            vts(X("LO", *hs), X("VI", *hs), PR - 1, A.bitwise_and)
            vcopy(X("LOL%d" % h, 0, 128), X("LO", *hs))
            ll = "LOL%d" % h
            db = ("PCa", "PCb")
            ds = [X("DS", 2048 * h + 512 * j, 2048 * h + 512 * j + 512) for j in range(4)]
            for j in range(4):
                if j == 3 and DV[t][h] == "V":
                    vcopy(ds[3], ind(win, X(ll, 96, 128)))
                else:
                    act(ds[j], ind(win, X(ll, 32 * j, 32 * j + 32)))
            for j in range(3):
                bank = db[(h + j) % 2]
                jj = j + (DV[t][h] == "S")
                mms([(X(bank, 0, 512), ID, ds[jj], True, True)])
                prev, nx = (ds[3] if DV[t][h] == "V" else ds[0]) if j == 0 else X(("DA", "DB")[j - 1], 0, 512), ("DA", "DB", "DC")[j]
                if j < 2:
                    vtt(X(nx, 0, 512), X(bank, 0, 512), prev, A.max)
            vtt(X("DC", 0, 256), X(bank, 0, 256), X("DB", 0, 256), A.max)
            vtt(X(bank, 256, 512), X(bank, 256, 512), X("DB", 256, 512), A.max)
            vtt(X("DE", 0, 128), X(bank, 256, 384), X("DC", 0, 128), A.max)
            vtt(X(bank, 0, 128), X(bank, 384, 512), X("DC", 128, 256), A.max)
            vtt(X("NEWP", 128 * h, 128 * h + 128), X(bank, 0, 128), X("DE", 0, 128), A.max)
            nw = X("NEWN", 128 * h, 128 * h + 128)
            vtt(nw, ind(X("NEWP", 128 * h, 128 * h + 128), X("NL3", 0, 8)), X("MSK%d" % t, h, 256, 2), A.add)
            if h == 0:
                vts(X("SEND%d" % t, 0, 128), nw, 255.0, A.min)
            vts(X("F", 16 + B + h, 16 + B + L, 2), nw, 255.0, A.min)

        for d in (1, 2, 3, 4):
            test(d, 0)
        largest(0)
        dst = T.cores[(rank + 1 + t % 7) % len(T.cores)]
        src = T.cores[(rank - 1 - t % 7) % len(T.cores)]
        es = topo.engines(core, dst)[:8]
        nsrc = len(topo.engines(src, core)[:8])
        rid, pid, _se = topo.addr(dst)
        mk = sum(1 << e for e in es)

        def send(e, t=t, cc=cc, rid=rid, pid=pid, mk=mk):
            e.remote_dma(out_ap=T.F[:, cc:cc + 128], in_ap=T["SEND%d" % t][:], remote_sem=T.sem["ar%d" % t],
                         local_sem=T.sem["lc%d" % t], pid=pid, routing_id=rid, dma_engine_mask=mk)

        rec("s", "G", [], [X("SEND%d" % t, 0, 128)], send, 0.3, 2.0, ("lc%d" % t, len(es)))
        rec("a", "R", [X("F", cc, cc + 128)], [X("SEND%d" % t, 0, 128)], None, 0.3, 2.0, ("ar%d" % t, nsrc))
        for d in (1, 2, 3, 4):
            test(d, 1)
        if t + 1 == R:
            come(t)
        largest(1)
        kr, kc = float(7 * PR + B + 16), float(6 * PR + B + L + 16)
        for h in (0, 1):
            hs = (128 * h, 128 * h + 128)
            hif, red = X("HIF", *hs), X("RED", *hs)
            pq = ("PQ0", "PG0")[h]
            vts(X("HI", *hs), X("VI", *hs), 13, A.arith_shift_right)
            vcopy(hif, X("HI", *hs))
            act(red, hif, AF.Relu, bias=1.0, scale=-1.0)
            act(X(pq, 0, 128), hif, AF.Relu, bias=kr, scale=-kr)
            act(X(pq, 128, 256), hif, AF.Relu, bias=-4.0 * kc, scale=kc)
            kk = [(128 * h + 8 * k, 128 * h + 8 * k + 8) for k in range(16)]
            o1, o2 = X(pq, 256, 264), X(pq, 264, 272)
            mms([(o1, NID, X("HIF", *c), n == 0, False) for n, c in enumerate(kk)]
                + [(o1, X("SU", 0, 128), X("RED", *c), False, n == 15) for n, c in enumerate(kk)]
                + [(o2, X("SU", 0, 128), X("RED", *c), n == 0, n == 15) for n, c in enumerate(kk)])
            e = X("E", *hs)
            vtt(e, ind(X("MI", 8 * h, 8 * h + 8), X("XL", 0, 8)), X("KEY", *hs), A.is_equal)
            vtt(X(pq, 384, 512), e, X("KS%d" % t, *hs), A.mult)
            xa = X("XA", 16 * h, 16 * h + 16)
            vcopy(xa, X(pq, 256, 272))
            q0 = 256 * h
            vtt(X("XY", q0, q0 + 256), ind(xa, X("XL", 0, 16)), X("K12", q0, q0 + 256), A.add)
            vts(X("XZ", q0, q0 + 128), X("XY", q0, q0 + 128), 255, A.bitwise_and)
            vts(X("XZ", q0 + 128, q0 + 256), X("XY", q0 + 128, q0 + 256), 127, A.bitwise_and)
            t1 = X("T1", *hs)
            vtt(X(pq, 256, 384), X(pq, 0, 128), X("XZ", q0, q0 + 128), A.add)
            vtt(t1, X(pq, 128, 256), X("XZ", q0 + 128, q0 + 256), A.add)
            vtt(t1, X(pq, 256, 384), t1, A.max)
            vtt(X(pq, 384, 512), X(pq, 384, 512), X("VI", *hs), A.max)
            vtt(X("NI", *hs), X(pq, 384, 512), t1, A.max)
            vts(X("NUM", *hs), X("NI", *hs), PR - 1, A.bitwise_and)
            if t + 1 < R:
                vcopy(X("PL", *hs), X("NUM", *hs))
                vts(X("CO0", *hs), X("NUM", *hs), float(5 * PR), A.add)
            else:
                vts(X("YPR", h, 256, 2), X("NUM", *hs), -16.0, A.add)
        if t + 1 == R:
            dma("Y", [], [X("YPR", 0, 256)], [(T.yp[k::16, :], T.YPR[:, 16 * k:16 * k + 16]) for k in range(16)])
        for h in (0, 1):
            act(X("PSP", 128 * h, 128 * h + 128), ind(X(pn, 2048 * h, 2048 * h + 2048), X("OFF%d" % h, 0, 8)))
        act(X("PSN", 0, 256), ind(X("PSP", 0, 256), X("NL", 0, 16)))
        grow("PSN", 256, 16 + B, NB * t, t, "PG1")
        y0 = NB * t
        dma("Y", [], [X("F", 16 + B, 16 + B + L)], [(T.yf[:, y0:y0 + L], T.F[:, 16 + B:16 + B + L])])
        dma("Y", [], [X("F", cc, cc + 128)], [(T.yf[:, y0 + L:y0 + NB], T.F[:, cc:cc + 128])])
        if t + 1 < R:
            come(t)

    def schedule():
        n = len(ops)
        pred = [set() for _ in range(n)]
        last = {}
        for i, o in enumerate(ops):
            for w, regs in ((0, o["r"]), (1, o["w"])):
                for (b, c0, c1, rows) in regs:
                    l = last.setdefault(b, [])
                    ps = b in PSUMS
                    for (j, w2, d0, d1, r2) in l:
                        if j != i and ((ps and ops[j]["q"] != o["q"]) or ((w or w2) and d0 < c1 and c0 < d1 and (rows & r2))):
                            pred[i].add(j)
                    if w and not ps:
                        l[:] = [x for x in l if not (x[2] >= c0 and x[3] <= c1 and (x[4] & ~rows) == 0)]
                    l.append((i, w, c0, c1, rows))
        succ = [[] for _ in range(n)]
        for i in range(n):
            for j in pred[i]:
                succ[j].append(i)
        prio = [0.0] * n
        for i in range(n - 1, -1, -1):
            prio[i] = ops[i]["cost"] + ops[i]["lat"] + max([prio[k] + WAKE for k in succ[i]] or [0.0])
        left = [len(p) for p in pred]
        ready = {}
        fin = [0.0] * n
        free = {}
        est = [0.0] * n
        for i in range(n):
            if not left[i]:
                ready.setdefault(ops[i]["q"], []).append(i)
        order = []
        while len(order) < n:
            best = None
            for q, l in ready.items():
                if not l:
                    continue
                f = free.get(q, 0.0)
                t0 = min(max(f, est[i]) for i in l)
                i = max((x for x in l if max(f, est[x]) <= t0 + 0.03), key=lambda x: prio[x])
                st = max(f, est[i])
                if best is None or st < best[0]:
                    best = (st, i, q)
            st, i, q = best
            ready[q].remove(i)
            order.append(i)
            free[q] = st + ops[i]["cost"]
            fin[i] = free[q] + ops[i]["lat"]
            for k in succ[i]:
                est[k] = max(est[k], fin[i] + WAKE)
                left[k] -= 1
                if not left[k]:
                    ready.setdefault(ops[k]["q"], []).append(k)
        return order

    eng = {"V": g.vector, "S": g.scalar, "T": g.tensor, "G": g, "Y": g.sync}
    sname = {"V": "sv", "S": "ss", "T": "st", "G": "sg"}
    cnt = {"V": 0, "S": 0, "T": 0, "G": 0}
    clk = {q: {} for q in "VSTGY"}
    log = {}
    total = {}
    ndma = [0]

    def waits(q, reads, writes):
        need = []
        for w, regs in ((0, reads), (1, writes)):
            for (b, c0, c1, rows) in regs:
                ps = b in PSUMS
                for e in log.get(b, []):
                    if ps and e["q"] != q:
                        need.append(e)
                        continue
                    if (ps and q == "T") or not (e["w"] or w) or e["c1"] <= c0 or e["c0"] >= c1 or not (e["rows"] & rows):
                        continue
                    if e["q"] == q and w and not e["w"]:
                        continue
                    need.append(e)
        want = {}
        for e in need:
            if clk[q].get(e["sem"], 0) < e["val"] and want.get(e["sem"], (0, None))[0] < e["val"]:
                want[e["sem"]] = (e["val"], e)
        for s in list(want):
            v = want[s][0]
            for s2 in want:
                if s2 != s and want[s2][1]["clk"].get(s, 0) >= v:
                    del want[s]
                    break
        for s, (v, e) in want.items():
            eng[q].wait_ge(T.sem[s], v)
            for a, b in e["clk"].items():
                clk[q][a] = max(clk[q].get(a, 0), b)
            clk[q][s] = max(clk[q].get(s, 0), v)

    def note(q, reads, writes, sem, val, c):
        c = dict(c)
        c[sem] = max(c.get(sem, 0), val)
        total[sem] = max(total.get(sem, 0), val)
        for w, regs in ((0, reads), (1, writes)):
            for (b, c0, c1, rows) in regs:
                l = log.setdefault(b, [])
                if b in PSUMS:
                    l[:] = [e for e in l if not (e["q"] == q and e["c0"] >= c0 and e["c1"] <= c1 and (w or not e["w"]))]
                elif w:
                    l[:] = [e for e in l if not (e["c0"] >= c0 and e["c1"] <= c1 and (e["rows"] & ~rows) == 0)]
                l.append({"q": q, "w": w, "c0": c0, "c1": c1, "rows": rows, "sem": sem, "val": val, "clk": c})

    if "order" not in ORDER:
        ORDER["order"] = schedule()
    for i in ORDER["order"]:
        o = ops[i]
        q, r, w = o["q"], o["r"], o["w"]
        if o["kind"] == "a":
            note("D", [], w, o["data"][0], o["data"][1], {})
            continue
        waits(q, r, w)
        if o["kind"] == "c":
            cnt[q] += 1
            o["fn"](eng[q]).then_inc(T.sem[sname[q]], 1)
            note(q, r, w, sname[q], cnt[q], clk[q])
        elif o["kind"] == "t":
            for (x, lh, rh, a, b) in o["data"]:
                cnt["T"] += 1
                g.tensor.matmul(x[0], lh[0], rh[0], a, b).then_inc(T.sem.st, 1)
            note("T", r, w, "st", cnt["T"], clk["T"])
        elif o["kind"] == "d":
            sem = "d%d" % ndma[0]
            ndma[0] += 1
            for (x, y) in o["data"]:
                eng[q].dma_start(x, y).then_inc(T.sem[sem], 16)
            note("D", r, w, sem, 16 * len(o["data"]), clk[q])
        else:
            o["fn"](g)
            note("D", r, w, o["data"][0], o["data"][1], clk["G"])
    for s, v in total.items():
        if clk["Y"].get(s, 0) < v:
            g.sync.wait_ge(T.sem[s], v)
